import numpy as np, ml_dtypes
CORES = [3,11,19,27,35,43,51,59]
N = 8
import mx_ref
BF = ml_dtypes.bfloat16
def gentries(a):
    return np.ascontiguousarray(a.reshape(8, 16, -1).transpose(0, 2, 1)).reshape(8, -1)
def gtable(e):
    e = np.asarray(e); return np.ascontiguousarray(e.reshape(8, -1, 16).transpose(0, 2, 1)).reshape(128, -1).astype(np.int32)
def gcols(t, e):
    v = np.concatenate([t.reshape(8, 16, -1, 4), np.zeros((8, 16, 1, 4), BF)], axis=2)
    return np.ascontiguousarray(np.stack([v[g][:, e[g]] for g in range(8)])).reshape(128, -1)
def tile(rs):
    return np.stack(rs, axis=2).reshape(128, -1).astype(BF)
def pick(q, e):
    c = np.concatenate([q[0].reshape(128, -1, 4), np.zeros((128, 1, 4), np.uint8)], axis=1); s = np.concatenate([q[1], np.ones((16, 1), np.uint8)], axis=1)
    return (np.ascontiguousarray(c[:, e].reshape(128, -1)), np.ascontiguousarray(s[:, e]))
def join(*qs):
    return (np.concatenate([q[0] for q in qs], axis=1), np.concatenate([q[1] for q in qs], axis=1))
def put(q, e, v):
    c, s = q[0].reshape(128, -1, 4).copy(), q[1].copy(); c[:, e] = v[0].reshape(128, -1, 4); s[:, e] = v[1]
    return (c.reshape(128, -1), s)
def pk(c, s):
    return (np.ascontiguousarray(c), mx_ref.live(s))
def emit(q):
    return q[0], q[1]
def packed(v, rng):
    q = [mx_ref.quantize(np.ascontiguousarray(v[r])) for r in range(N)]
    return np.stack([a for a, b in q]), np.stack([mx_ref.plane(b, rng) for a, b in q])
def values_of_codes():
    e, c = np.zeros((128, 128, 4), np.float32), np.zeros((128, 2, 4), np.uint8)
    e[np.arange(128), np.arange(128), 0] = 1
    c[:127, :, 0] = np.arange(256).reshape(2, 128).T[:127]
    return mx_ref.matmul(mx_ref.quantize(e.reshape(128, 512).astype(BF)), (c.reshape(128, 8), np.full((16, 2), 127, np.uint8))).T.reshape(-1).astype(np.float64)
CODE_VALUE, SCALE_VALUE = values_of_codes(), 2.0 ** (np.arange(256) - 127.0)
def decode(q):
    return (CODE_VALUE[q[0]].reshape(16, 8, -1, 4) * SCALE_VALUE[q[1]][:, None, :, None] + 0.0).reshape(128, -1).astype(np.float32)
def f(rng, *shape):
    return mx_ref.flush((rng.standard_normal(shape, dtype=np.float32) * np.exp2(rng.integers(-2, 3, shape[:-1] + (1,)))).astype(BF))
def wide(rng, *shape, cols=0):
    v = rng.standard_normal(shape, dtype=np.float32) * np.exp2(rng.integers(-12, 13, shape)).astype(np.float32)
    if cols: v *= np.repeat(np.exp2(rng.integers(-cols, cols + 1, shape[:-2] + (1, shape[-1] // 4))) * (rng.random(shape[:-2] + (1, shape[-1] // 4)) > 0.0625), 4, axis=-1).astype(np.float32)
    return mx_ref.flush(v.astype(BF))
C, K, A, B, R = 256, 64, 4, 4, 3
STEP = [1, 2, 4]
def classes(key):
    c, one, two = np.zeros((8, C), int), np.full((8, K), -1), np.full((8, K), -1)
    for g in range(8):
        first, mine = np.unique(key[g], return_index=True, return_inverse=True)[1:]
        low = np.sort(first)
        c[g] = np.searchsorted(low, first[mine])
        for k in range(len(low)):
            m = np.flatnonzero(c[g] == k)
            one[g, k] = m[0]
            two[g, k] = m[min(1, len(m) - 1)]
    return c, one, two
def numbers_of(rng):
    return {"x": np.array(f(rng, N, 128, 4 * C)), "u": np.array(f(rng, N, 128, 512)), "v": np.array(f(rng, N, 128, 512))}
def lists_of(rng):
    return {"nx": rng.integers(0, C, (N, 8, C)), "co": rng.integers(0, K, (N, 8, C))}
def stored(l):
    return {k: np.stack([gtable(e) for e in l[k]]) for k in ("nx", "co")}
def weights(rng, w):
    c, p = packed(w, rng)
    return {"wc": c, "ws": p}
def quiet(rng):
    w = np.array(f(rng, N, 128, 2048)).reshape(N, 8, 16, 4, 8, 16, 4)
    w[:, :, :8] = 0
    w[:, :, :, :, :, :8] = 0
    return weights(rng, w.reshape(N, 128, 2048))
def marked(d, m, k):
    x = d["x"].reshape(N, 8, 16, C, 4)
    u = d["u"].reshape(N, 128, 128, 4)
    x[:, :, :8] = 0
    k = k.astype(np.float32)
    for i in range(2):
        x[:, :, i, :, :2] = m[:, :, :, i].astype(np.float32).astype(BF)
        u[:, :, i::16] = 0
        for h in range(i, 128, 16):
            u[:, h, h, 0] = k.astype(BF)
            u[:, h, h, 1] = (-k).astype(BF)
    return {"x": x.reshape(N, 128, 4 * C), "u": u.reshape(N, 128, 512), "v": d["v"]}
def setup_inputs(rng):
    return {**numbers_of(rng), **stored(lists_of(rng)), **weights(rng, f(rng, N, 128, 2048))}
def setup_inputs_full(rng):
    d, l = numbers_of(rng), lists_of(rng)
    o = rng.permutation(N)
    bits = np.zeros((N, 8, C), int)
    for r in range(N):
        e = np.argsort(rng.random((8, C)), axis=1)
        if o[r] % 4 == 3:
            l["co"][r] = rng.integers(0, K, (8, 1))
            bits[r] = e % (1 + rng.permutation(8) % 4)[:, None]
        else:
            k, one, two = classes(np.minimum(e, K - 1) if o[r] % 4 == 1 else e % K)
            l["co"][r] = k % A + A * rng.integers(0, K // A, (8, C))
            l["nx"][r] = np.take_along_axis(one, k // A % B + B * rng.integers(0, K // B, (8, C)), axis=1)
            bits[r] = k // (A * B)
    m = np.zeros((N, 8, C, 2, 2))
    m[:, :, :, 0] = 2 * (np.arange(2) == (bits >> 1)[:, :, :, None])
    m[:, :, :, 1] = 2 * (np.arange(2) == (bits & 1)[:, :, :, None])
    return {**marked(d, m, np.ones(N)), **stored(l), **quiet(rng)}
def setup_inputs_near(rng):
    d, l = numbers_of(rng), lists_of(rng)
    p = np.array([[0, 0], [2, 2], [3, 2], [2, 3], [2, 0], [0, 2]])
    e = np.argsort(rng.random((N, 8, C)), axis=2)
    h = np.argsort(rng.random((N, 8, C)), axis=2)
    m = np.stack([p[e // 4 % 6], p[h % 6]], axis=3) * 2.0 ** np.array([-30, -12, 0, 28])[e % 4][:, :, :, None, None]
    k = np.where(rng.permutation(N) < N // 2, 2.0 ** -30, 1.0)
    return {**marked(d, m, k), **stored(l), **quiet(rng)}
def setup_inputs_lists(rng):
    d, l = numbers_of(rng), lists_of(rng)
    o = rng.permutation(N)
    x = d["x"].reshape(N, 128, C, 4)
    for r in range(N):
        a = x[r][:, :2].copy()
        if o[r] % 4 == 0: l["nx"][r] = np.arange(C)
        if o[r] % 4 == 1: l["nx"][r] = rng.integers(0, C, (8, 1))
        if o[r] % 4 == 2:
            l["nx"][r] = C - 1 - np.arange(C)
            a[:, 1] = 0
            x[r] = a[:, rng.permutation(C) % 2]
        if o[r] % 4 == 3:
            l["co"][r] = rng.integers(0, K, (8, 1))
            x[r] = a[:, np.zeros(C, int)]
    return {"x": x.reshape(N, 128, 4 * C), "u": d["u"], "v": d["v"], **stored(l), **weights(rng, f(rng, N, 128, 2048))}
def setup_inputs_huge(rng):
    d, l = numbers_of(rng), lists_of(rng)
    o = rng.permutation(N)
    c = np.stack([rng.permutation(C) % 2 * 2.0 - 1.0 for r in range(N)])
    c[o == 0] = 1
    c[o == 1] = -1
    p = rng.random((N, 128, C, 4))
    x = np.where(c[:, None, :, None] < 0, -2.0 ** 30 * (1 - 0.125 * p), 2.0 ** 28 * (1 - 0.5 * p))
    k = np.stack([rng.permutation(8) % 4 for r in range(N)])
    s = 1.0 - 2.0 * np.stack([k >> 1, k & 1], axis=2)
    u = d["u"].reshape(N, 128, 8, 16, 4)
    a = 2.0 ** 30 * (1 - 0.25 * rng.random((N, 128, 8, 2, 4))) * s[:, None, :, :, None]
    u[:, :, :, :2] = a.astype(np.float32).astype(BF)
    w = np.zeros((N, 128, 4, 128, 4), np.float32)
    i = np.arange(128)
    for b in range(4): w[:, i, b, i, b] = 8
    return {"x": x.astype(np.float32).reshape(N, 128, 4 * C).astype(BF), "u": u.reshape(N, 128, 512), "v": d["v"], **stored(l), **weights(rng, w.reshape(N, 128, 2048).astype(BF))}
def setup_inputs_spread(rng):
    d = setup_inputs(rng)
    d["x"] = wide(rng, N, 128, 4 * C, cols=6)
    return d
def check_inputs(d):
    b = []
    for k in ("x", "u", "v"):
        a = np.abs(d[k].astype(np.float32))
        if not (np.isfinite(a).all() and ((a == 0) | (a >= 2.0 ** -30) & (a <= 2.0 ** 30)).all()): b.append("a value of " + k)
    if ((d["nx"] < 0) | (d["nx"] >= C)).any(): b.append("an entry of nx")
    if ((d["co"] < 0) | (d["co"] >= K)).any(): b.append("an entry of co")
    if ((d["wc"] == 0x7F) | (d["wc"] == 0xFF)).any(): b.append("a code of wc is no number")
    for r in range(N):
        s = mx_ref.live(d["ws"][r])
        if ((s > 1) & (s < 64) | (s > 191)).any(): b.append("a scale of ws")
    return b
def reference(x, u, v, nx, co, wc, ws):
    qu = [mx_ref.quantize(u[r]) for r in range(N)]
    lay = [pk(wc[r], ws[r]) for r in range(N)]
    now = [x[r] for r in range(N)]
    to = [gentries(nx[r]).astype(np.int64) for r in range(N)]
    cl = [gentries(co[r]).astype(np.int64) for r in range(N)]
    for t in range(R):
        held, sent = [], []
        for r in range(N):
            q = mx_ref.quantize(now[r])
            held.append(decode(q).astype(BF))
            neg = mx_ref.matmul(qu[r], q) + np.float32(0.0) < 0
            key = 4 * B * (cl[r] % A) + 4 * (np.take_along_axis(cl[r], to[r], axis=1) % B) + 2 * neg[::16] + neg[1::16]
            cl[r], one, two = classes(key)
            z = (gcols(held[r], one).astype(np.float32) + gcols(held[r], two).astype(np.float32)) * np.float32(0.5)
            sent.append(mx_ref.quantize(z.astype(BF)))
        for r in range(N):
            e = (r + STEP[t]) % N
            h = tile([np.maximum(mx_ref.matmul(pick(lay[e], np.arange(128 * b, 128 * b + 128)), sent[r]), np.float32(0.0)) * np.float32(0.03125) for b in range(4)])
            came = decode(mx_ref.quantize(h)).astype(BF)
            now[r] = (held[r].astype(np.float32) + gcols(came, cl[r]).astype(np.float32)).astype(BF)
    y, ol = np.zeros((N, 128, C), np.float32), np.zeros((N, 8, C), np.float32)
    oc, osc = np.zeros((N, 128, 4 * C), np.uint8), np.zeros((N, 16, C), np.uint8)
    for r in range(N):
        q = mx_ref.quantize(now[r])
        y[r] = mx_ref.matmul(mx_ref.quantize(v[r]), q)
        ol[r] = cl[r]
        oc[r], osc[r] = emit(q)
    return {"y": y, "ol": ol, "oc": oc, "osc": osc}

@@ -1,0 +1,367 @@
+from concourse.bass import DstId, RemoteDMATransfer
+from concourse.mybir import dt, AluOpType, AxisListType, ActivationFunctionType
+
+C, K, R = 256, 64, 3
+STEP = [1, 2, 4]
+PL = C + K
+CODES = "float8_e4m3fn_x4"
+
+SCRATCH = {
+    "ones": ("sbuf", [128, 516], "bfloat16"), "strip": ("sbuf", [128, 516], "bfloat16"), "zero": ("sbuf", [128, 512], "bfloat16"),
+    "eq": ("sbuf", [128, 512], CODES), "esc": ("sbuf", [128, 512], "uint8"),
+    "ut": ("sbuf", [128, 512], "bfloat16"), "qu": ("sbuf", [128, 128], CODES), "su": ("sbuf", [128, 128], "uint8"),
+    "uu": ("sbuf", [128, 256], CODES), "us": ("sbuf", [128, 256], "uint8"),
+    "vt": ("sbuf", [128, 512], "bfloat16"), "qv": ("sbuf", [128, 128], CODES), "sv": ("sbuf", [128, 128], "uint8"),
+    "wq": ("sbuf", [128, 512], CODES), "wp": ("sbuf", [128, 512], "uint8"),
+    "nxi": ("sbuf", [128, 16], "int32"), "coi": ("sbuf", [128, 16], "int32"),
+    "nxo": ("sbuf", [128, 16], "uint16"), "coo": ("sbuf", [128, 16], "uint16"),
+    "uoi": ("sbuf", [128, 16], "int32"), "uoo": ("sbuf", [128, 16], "uint16"),
+    "iot": ("sbuf", [128, 320], "float32"), "mi": ("sbuf", [128, 64], "int32"), "mi3": ("sbuf", [128, 64], "int32"),
+    "m4t": ("sbuf", [128, 64], "bfloat16"),
+    "pi": ("sbuf", [128, 4], "int32"), "p15": ("sbuf", [128, 4], "int32"), "p16": ("sbuf", [128, 4], "int32"),
+    "si": ("sbuf", [128, 4], "int32"), "kap": ("sbuf", [128, 4], "float32"), "kv": ("sbuf", [128, 4], "float32"),
+    "lo": ("sbuf", [128, 1], "float32"), "hi": ("sbuf", [128, 1], "float32"),
+    "flr": ("sbuf", [128, 272], "bfloat16"),
+    "fh": ("sbuf", [128, 4 * PL], "bfloat16"), "fs": ("sbuf", [128, 512], "bfloat16"),
+    "sa": ("sbuf", [128, 256], "bfloat16"), "sb": ("sbuf", [128, 256], "bfloat16"), "k1": ("sbuf", [128, 256], "bfloat16"),
+    "pk": ("sbuf", [128, 256], "bfloat16"), "cm4": ("sbuf", [128, 256], "bfloat16"), "cm16": ("sbuf", [128, 256], "bfloat16"),
+    "kr": ("sbuf", [128, 288], "bfloat16"), "cr": ("sbuf", [128, 288], "bfloat16"),
+    "ta": ("sbuf", [128, 256], "bfloat16"), "tb": ("sbuf", [128, 288], "bfloat16"),
+    "e1": ("sbuf", [128, 32], "float32"), "kwf": ("sbuf", [128, 16], "float32"),
+    "kw": ("sbuf", [128, 16], "uint16"), "cw": ("sbuf", [128, 16], "uint16"),
+    "junk": ("sbuf", [128, 4 * 272], "bfloat16"), "jun2": ("sbuf", [128, 256], "float32"),
+    "vv": ("sbuf", [128, 4], "float32"), "acc": ("sbuf", [128, 4], "float32"), "fr": ("sbuf", [128, 64], "float32"),
+    "f16": ("sbuf", [128, 4], "uint16"), "s16": ("sbuf", [128, 4], "uint16"), "off": ("sbuf", [128, 16], "uint16"),
+    "fi": ("sbuf", [128, 4], "int32"), "sd": ("sbuf", [128, 24], "float32"),
+    "g1": ("sbuf", [128, 256], "bfloat16"), "zk": ("sbuf", [128, 256], "bfloat16"),
+    "zt": ("sbuf", [128, 512], "bfloat16"), "ht": ("sbuf", [128, 512], "bfloat16"),
+    "ri": ("sbuf", [128, 64], "int32"), "rm": ("sbuf", [128, 64], "int32"), "rm4": ("sbuf", [128, 64], "bfloat16"),
+    "dh": ("sbuf", [128, 256], "bfloat16"), "g2": ("sbuf", [128, 512], "bfloat16"),
+    "cf": ("sbuf", [128, 256], "float32"), "yo": ("sbuf", [128, 256], "float32"),
+    "pf": ("psum", [128, 2048], "float32"), "pw": ("psum", [128, 2048], "float32"),
+}
+for _i in range(4):
+    SCRATCH["m%d" % _i] = ("sbuf", [128, 272], "bfloat16")
+    SCRATCH["w%d" % _i] = ("sbuf", [128, 272], "bfloat16")
+    SCRATCH["t%d" % _i] = ("sbuf", [128, 1024], "bfloat16")
+    SCRATCH["q%d" % _i] = ("sbuf", [128, 256], CODES)
+    SCRATCH["s%d" % _i] = ("sbuf", [128, 256], "uint8")
+for _i in range(R):
+    for _n in "zh":
+        SCRATCH["%sq%d" % (_n, _i)] = ("sbuf", [128, 256], CODES)
+        SCRATCH["%ss%d" % (_n, _i)] = ("sbuf", [128, 256], "uint8")
+        SCRATCH["%sc%d" % (_n, _i)] = ("sbuf", [128, 192], CODES)
+        SCRATCH["%sp%d" % (_n, _i)] = ("sbuf", [128, 384], "uint8")
+
+DMAS = ["dx", "du", "dv", "dwc", "dws", "dn", "dc", "dol", "dy0", "dy1", "doc", "ds0", "ds1", "ds2", "ds3"]
+SEMAPHORES = ["cv", "cs", "ct", "cg", "left"] + ["za%d" % i for i in range(R)] + ["ha%d" % i for i in range(R)] + DMAS
+
+
+def rank_program(g, core, T, topo):
+    rank = T.rank_of(core)
+    if rank is None:
+        return
+    add, sub, mult, amax = AluOpType.add, AluOpType.subtract, AluOpType.mult, AluOpType.max
+    F = ActivationFunctionType
+    eng = {"v": g.vector, "s": g.scalar, "t": g.tensor, "g": g, "y": g.sync}
+    count = {"cv": 0, "cs": 0, "ct": 0, "cg": 0, "left": 0}
+    known = {q: {} for q in eng}
+    wrote, read = {}, {}
+
+    def over(book, reg):
+        return [e for e in book.get(reg[0], []) if e[0] < reg[2] and reg[1] < e[1]]
+
+    def need(q, reads, writes):
+        want = {}
+        for reg in reads:
+            for e in over(wrote, reg):
+                want[e[3]] = max(want.get(e[3], 0), e[4])
+            if reg[0] in ("pf", "pw"):
+                for e in over(read, reg):
+                    if e[2] != q:
+                        want[e[3]] = max(want.get(e[3], 0), e[4])
+        for reg in writes:
+            for e in over(wrote, reg):
+                want[e[3]] = max(want.get(e[3], 0), e[4])
+            for e in over(read, reg):
+                if e[2] != q:
+                    want[e[3]] = max(want.get(e[3], 0), e[4])
+        for s in sorted(want):
+            if known[q].get(s, 0) < want[s]:
+                eng[q].wait_ge(T.sem[s], want[s])
+                known[q][s] = want[s]
+
+    def note(q, reads, writes, s, n):
+        for reg in writes:
+            for book in (wrote, read):
+                book[reg[0]] = [e for e in book.get(reg[0], []) if not (reg[1] <= e[0] and e[1] <= reg[2])]
+            wrote[reg[0]].append((reg[1], reg[2], q, s, n))
+        for reg in reads:
+            book = [e for e in read.get(reg[0], []) if not (e[2] == q and reg[1] <= e[0] and e[1] <= reg[2])]
+            book.append((reg[1], reg[2], q, s, n))
+            read[reg[0]] = book
+
+    def op(q, call, reads, writes):
+        need(q, reads, writes)
+        s = "c" + q
+        count[s] += 1
+        call().then_inc(T.sem[s], 1)
+        note(q, reads, writes, s, count[s])
+
+    def dma(q, s, out, in_, reads, writes):
+        need(q, reads, writes)
+        eng[q].dma_start(out, in_).then_inc(T.sem[s], 16)
+        note(q, reads, writes, s, 16)
+
+    V, S, PE = g.vector, g.scalar, g.tensor
+
+    def r(name, a=0, b=None):
+        return (name, a, T[name].shape[1] if b is None else b)
+
+    def quant(qb, sb_, tile, a, n, c0=0):
+        op("v", lambda: V.quantize_mx(T[qb][:, a:a + n], T[sb_][:, a:a + n], T[tile][:, 4 * c0:4 * (c0 + n)]),
+           [(tile, C * b + c0, C * b + c0 + n) for b in range(4)] if tile in ("t1", "t2", "t3") else [r(tile)],
+           [r(qb, a, a + n), r(sb_, a, a + n)])
+
+    def fill(name, a, b, val):
+        op("v", lambda: V.memset(T[name][:, a:b], val), [], [r(name, a, b)])
+
+    def ts(out, in0, s1, s2, op0, op1, reads, writes):
+        if s2 is None:
+            op("v", lambda: V.tensor_scalar(out, in0, s1, None, op0), reads, writes)
+        else:
+            op("v", lambda: V.tensor_scalar(out, in0, s1, s2, op0, op1), reads, writes)
+
+    def tt(out, a, b, o, reads, writes):
+        op("v", lambda: V.tensor_tensor(out, a, b, o), reads, writes)
+
+    def cp(out, a, reads, writes):
+        op("v", lambda: V.tensor_copy(out, a), reads, writes)
+
+    def act(out, a, f, reads, writes, **kw):
+        op("s", lambda: S.activation(out, a, f, **kw), reads, writes)
+
+    def mm(bank, buf, n, lq, ls, la, rq, rs, ra):
+        op("t", lambda: PE.matmul_mx(T[buf][:, 512 * bank:512 * bank + n], T[lq][:, la:la + 128], T[ls][:, la:la + 128],
+                                     T[rq][:, ra:ra + n], T[rs][:, ra:ra + n], True, True),
+           [r(lq, la, la + 128), r(ls, la, la + 128), r(rq, ra, ra + n), r(rs, ra, ra + n)], [(buf, 512 * bank, 512 * bank + 512)])
+
+    def bank(buf, b):
+        return (buf, 512 * b, 512 * b + 512)
+
+    def send(kind, t, peer):
+        cq, sq = kind + "q%d" % t, kind + "s%d" % t
+        need("g", [r(cq, 0, 64), r(sq)], [])
+        dst = T.cores[peer]
+        rid, pid, _se = topo.addr(dst)
+        e = topo.engines(core, dst)
+        half = len(e) // 2
+        arr = T.sem[kind + "a%d" % t]
+        tr = [RemoteDMATransfer(dst_ids=[DstId(rid=rid, pnc=pid)], dma_engine_mask=sum(1 << k for k in e[:half]), remote_sem=arr,
+                                src=T[cq][:, 0:64].bitcast(dt.uint8), dst=T[kind + "c%d" % t][:, 128:192].bitcast(dt.uint8)),
+              RemoteDMATransfer(dst_ids=[DstId(rid=rid, pnc=pid)], dma_engine_mask=sum(1 << k for k in e[half:]), remote_sem=arr,
+                                src=T[sq][:, 0:256], dst=T[kind + "p%d" % t][:, 128:384])]
+        g.remote_dma_fused(tr, local_sem=T.sem.left)
+        count["left"] += len(e)
+
+    def arrival(kind, t, peer):
+        n = len(topo.engines(T.cores[peer], core))
+        note("r", [], [(kind + "c%d" % t, 128, 192), (kind + "p%d" % t, 128, 384)], kind + "a%d" % t, n)
+
+    def pads(t):
+        for k in "zh":
+            quant(k + "q%d" % t, k + "s%d" % t, "zero", 128, 128)
+            quant(k + "c%d" % t, k + "p%d" % t, "zero", 0, 128)
+
+    def as_list(row, dest, scale, base):
+        op("v", lambda: V.transpose(T.ta[:, 0:256], T[row][:, 16:272]), [r(row)], [r("ta")])
+        op("v", lambda: V.transpose(T.tb[:, 0:288], T[row][:, 0:288]), [r(row)], [r("tb")])
+        for k, (src, a, m) in enumerate((("ta", 0, "lo"), ("ta", 16, "hi"), ("tb", 16, "hi"), ("tb", 32, "lo"))):
+            end = 288 if a == 32 else 256
+            ts(T.e1[:, 8 * k:8 * k + 8], T[src][:, a:end:32], T[m][:, 0:1], None, mult, None, [r(src), r(m)], [r("e1", 8 * k, 8 * k + 8)])
+        tt(T.kwf[:, 0:16:2], T.e1[:, 0:8], T.e1[:, 16:24], add, [r("e1", 0, 8), r("e1", 16, 24)], [("kwf", 0, 8)])
+        tt(T.kwf[:, 1:16:2], T.e1[:, 8:16], T.e1[:, 24:32], add, [r("e1", 8, 16), r("e1", 24, 32)], [("kwf", 8, 16)])
+        ts(T[dest][:, 0:16], T.kwf[:, 0:16], scale, base, mult, add, [r("kwf")], [r(dest)])
+
+    def prekeys():
+        ts(T.cm16[:, 0:256], T.cm4[:, 0:256], 4.0, 2.0, mult, add, [r("cm4")], [r("cm16")])
+        tt(T.pk[:, 0:256], T.cm4[:, 0:256].indirect(T.nxo[:, 0:16]), T.cm16[:, 0:256], add, [r("cm4"), r("nxo"), r("cm16")], [r("pk")])
+
+    dma("y", "dx", T.t0[:], T.x[:], [], [r("t0")])
+    dma("s", "dc", T.coi[:], T.co[:], [], [r("coi")])
+    dma("s", "dn", T.nxi[:], T.nx[:], [], [r("nxi")])
+    dma("s", "du", T.ut[:], T.u[:], [], [r("ut")])
+    fill("ones", 0, 516, 1.0)
+    op("g", lambda: g.iota(T.mi[:, 0:64], [[1, 64]], 0, 0), [], [r("mi")])
+    op("g", lambda: g.iota(T.pi[:, 0:4], [[0, 4]], 0, 1), [], [r("pi")])
+    op("g", lambda: g.iota(T.si[:, 0:4], [[16, 4]], 0, 0), [], [r("si")])
+    op("g", lambda: g.affine_select(T.strip[:, 0:516], T.ones[:, 0:516], [[-1, 516]], AluOpType.is_equal, 0.0, 3, 4), [r("ones")], [r("strip")])
+    op("g", lambda: g.iota(T.uoi[:, 0:16], [[1, 2], [16, 8]], 0, 0), [], [r("uoi")])
+    op("g", lambda: g.iota(T.iot[:, 0:320], [[1, 320]], 0, 0, allow_small_or_imprecise_dtypes=True), [], [r("iot")])
+    fill("zero", 0, 512, 0.0)
+    ts(T.mi3[:, 0:64], T.mi[:, 0:64], 3, None, AluOpType.bitwise_and, None, [r("mi")], [r("mi3")])
+    ts(T.m4t[:, 0:64], T.mi3[:, 0:64], 4.0, None, mult, None, [r("mi3")], [r("m4t")])
+    ts(T.p15[:, 0:4], T.pi[:, 0:4], 15, None, AluOpType.bitwise_and, None, [r("pi")], [r("p15")])
+    tt(T.kap[:, 0:4], T.p15[:, 0:4], T.si[:, 0:4], add, [r("p15"), r("si")], [r("kap")])
+    ts(T.kv[:, 0:4], T.kap[:, 0:4], 2.0, -63.0, mult, add, [r("kap")], [r("kv")])
+    for i in range(4):
+        cp(T["m%d" % i][:, 256:257], T.kap[:, i:i + 1], [r("kap")], [r("m%d" % i, 256, 257)])
+        fill("w%d" % i, 257, 258, 0.0625)
+        fill("fh", PL * i + C, PL * i + PL, 0.0)
+    fill("flr", 0, 272, 2.0 ** -20)
+    fill("zt", 256, 512, 0.0)
+    cp(T.coo[:, 0:16], T.coi[:, 0:16], [r("coi")], [r("coo")])
+    cp(T.nxo[:, 0:16], T.nxi[:, 0:16], [r("nxi")], [r("nxo")])
+    act(T.cm4[:, 0:256], T.m4t[:, 0:64].indirect(T.coo[:, 0:16]), F.Copy, [r("m4t"), r("coo")], [r("cm4")])
+    for b in range(4):
+        op("v", lambda: V.quantize_mx(T.eq[:, 128 * b:128 * b + 128], T.esc[:, 128 * b:128 * b + 128], T.strip[:, 3 - b:515 - b]),
+           [r("strip")], [r("eq", 128 * b, 128 * b + 128), r("esc", 128 * b, 128 * b + 128)])
+    cp(T.uoo[:, 0:16], T.uoi[:, 0:16], [r("uoi")], [r("uoo")])
+    quant("zq0", "zs0", "zero", 128, 128)
+    prekeys()
+    quant("qu", "su", "ut", 0, 128)
+    cp(T.uu[:, 0:256].bitcast(dt.uint32), T.qu[:, 0:128].bitcast(dt.uint32).indirect(T.uoo[:, 0:16]), [r("qu"), r("uoo")], [r("uu")])
+    act(T.us[:, 0:256], T.su[:, 0:128].indirect(T.uoo[:, 0:16]), F.Copy, [r("su"), r("uoo")], [r("us")])
+    need("y", [r("t0")], [])
+    dma("y", "dwc", T.wq[:, 0:512].bitcast(dt.uint8), T.wc[:, 0:2048], [], [r("wq")])
+    dma("y", "dws", T.wp[:, 0:512], T.ws[:, 0:512], [], [r("wp")])
+    dma("y", "dv", T.vt[:], T.v[:], [], [r("vt")])
+    for h in range(2):
+        quant("q0", "s0", "t0", 128 * h, 128, 128 * h)
+
+    for t in range(R):
+        q, s = "q%d" % t, "s%d" % t
+        to, frm = (rank + STEP[t]) % len(T.cores), (rank - STEP[t]) % len(T.cores)
+        for h in range(2):
+            for k in range(2):
+                mm(2 * h + k, "pw", 128, "uu", "us", 128 * k, q, s, 128 * h)
+        for b in range(4):
+            mm(b, "pf", 256, "eq", "esc", 128 * b, q, s, 0)
+        for h in range(2):
+            a, e = 128 * h, 128 * h + 128
+            for k, n in enumerate(("sa", "sb")):
+                act(T[n][:, a:e], T.pw[:, 1024 * h + 512 * k:1024 * h + 512 * k + 128], F.Sign, [bank("pw", 2 * h + k)], [r(n, a, e)],
+                    bias=-1e-36, scale=-1.0)
+            tt(T.k1[:, a:e], T.sa[:, a:e], T.pk[:, a:e], add, [r("sa", a, e), r("pk", a, e)], [r("k1", a, e)])
+            tt(T.kr[:, 16 + a:16 + e], T.k1[:, a:e], T.sb[:, a:e], mult, [r("k1", a, e), r("sb", a, e)], [r("kr", 16 + a, 16 + e)])
+
+        def half_f(b):
+            act(T.fh[:, PL * b:PL * b + C], T.pf[:, 512 * b:512 * b + C], F.Copy, [bank("pf", b)], [r("fh", PL * b, PL * b + C)], scale=0.5)
+
+        def mask(i):
+            ts(T["m%d" % i][:, 0:256], T.kr[:, 16:272], T.kv[:, i:i + 1], 2.0 ** -10, AluOpType.not_equal, amax,
+               [r("kr", 16, 272), r("kv")], [r("m%d" % i, 0, 256)])
+
+        def scan(i):
+            op("v", lambda: V.tensor_tensor_scan(T["w%d" % i][:, 0:257], T["m%d" % i][:, 0:257], T.flr[:, 0:257], 1.0, mult, amax),
+               [r("m%d" % i, 0, 257), r("flr")], [r("w%d" % i, 0, 257)])
+            if i < 3:
+                act(T.junk[:, 272 * i:272 * i + 258], T["w%d" % i][:, 0:258], F.Copy, [r("w%d" % i, 0, 258)],
+                    [r("junk", 272 * i, 272 * i + 272), r("vv", i, i + 1)], accum_out=T.vv[:, i:i + 1])
+            else:
+                op("v", lambda: V.tensor_reduce(T.vv[:, 3:4], T.w3[:, 0:258], AxisListType.X, add), [r("w3", 0, 258)], [r("vv", 3, 4)])
+        half_f(0)
+        half_f(1)
+        mask(0)
+        mask(1)
+        scan(0)
+        mask(2)
+        scan(1)
+        mask(3)
+        scan(2)
+        scan(3)
+        half_f(2)
+        half_f(3)
+        cp(T.f16[:, 0:4], T.vv[:, 0:4], [r("vv")], [r("f16")])
+        cp(T.fr[:, 0:64], T.iot[:, 0:320].indirect(T.f16[:, 0:4]), [r("iot"), r("f16")], [r("fr")])
+        for i in range(4):
+            act(T.jun2[:, 64 * i:64 * i + 64], T.fr[:, 0:64], F.Sign, [r("fr"), r("vv")], [r("jun2", 64 * i, 64 * i + 64), r("acc", i, i + 1)],
+                bias=T.vv[:, i:i + 1], scale=-1.0, accum_out=T.acc[:, i:i + 1])
+        for b in range(4):
+            act(T.g1[:, 64 * b:64 * b + 64], T.fh[:, PL * b:PL * b + PL].indirect(T.f16[:, 0:4]), F.Copy,
+                [r("fh", PL * b, PL * b + PL), r("f16")], [r("g1", 64 * b, 64 * b + 64)])
+        cp(T.fi[:, 0:4], T.vv[:, 0:4], [r("vv")], [r("fi")])
+        tt(T.sd[:, 0:4], T.vv[:, 0:4], T.fi[:, 0:4], sub, [r("vv"), r("fi")], [r("sd", 0, 4)])
+        ts(T.sd[:, 4:8], T.sd[:, 0:4], 1024.0, -63.875, mult, add, [r("sd", 0, 4)], [r("sd", 4, 8)])
+        tt(T.sd[:, 8:12], T.sd[:, 4:8], T.fi[:, 0:4], add, [r("sd", 4, 8), r("fi")], [r("sd", 8, 12)])
+        ts(T.sd[:, 12:16], T.sd[:, 8:12], 255.7, None, AluOpType.is_lt, None, [r("sd", 8, 12)], [r("sd", 12, 16)])
+        tt(T.sd[:, 16:20], T.sd[:, 12:16], T.sd[:, 4:8], mult, [r("sd", 4, 8), r("sd", 12, 16)], [r("sd", 16, 20)])
+        tt(T.sd[:, 20:24], T.sd[:, 16:20], T.fi[:, 0:4], add, [r("sd", 16, 20), r("fi")], [r("sd", 20, 24)])
+        cp(T.s16[:, 0:4], T.sd[:, 20:24], [r("sd", 20, 24)], [r("s16")])
+        for b in range(4):
+            ts(T.off[:, 4 * b:4 * b + 4], T.acc[:, 0:4], 2.0, 124.0 + b, mult, add, [r("acc")], [r("off", 4 * b, 4 * b + 4)])
+        for b in range(4):
+            tt(T.zk[:, 64 * b:64 * b + 64], T.fh[:, PL * b:PL * b + PL].indirect(T.s16[:, 0:4]), T.g1[:, 64 * b:64 * b + 64], add,
+               [r("fh", PL * b, PL * b + PL), r("s16"), r("g1", 64 * b, 64 * b + 64)], [r("zk", 64 * b, 64 * b + 64)])
+        cp(T.zt[:, 0:256].indirect(T.off[:, 0:16]), T.zk[:, 0:256], [r("zk"), r("off")], [r("zt", 0, 256)])
+        quant("zq%d" % t, "zs%d" % t, "zt", 0, 128)
+        send("z", t, to)
+        arrival("z", t, frm)
+        for b in range(2):
+            act(T.fs[:, C * b:C * b + C], T.pf[:, 512 * b:512 * b + C], F.Copy, [bank("pf", b)], [r("fs", C * b, C * b + C)])
+        if t == 0:
+            ts(T.p16[:, 0:4], T.pi[:, 0:4], 16, None, AluOpType.bitwise_and, None, [r("pi")], [r("p16")])
+            ts(T.hi[:, 0:1], T.p16[:, 0:1], 0.0625, None, mult, None, [r("p16")], [r("hi")])
+            ts(T.lo[:, 0:1], T.p16[:, 0:1], -0.0625, 1.0, mult, add, [r("p16")], [r("lo")])
+            for n in ("kr", "cr"):
+                fill(n, 0, 16, 0.0)
+                fill(n, 272, 288, 0.0)
+            quant("zc0", "zp0", "zero", 0, 128)
+        ts(T.ri[:, 0:64], T.iot[:, 0:320].indirect(T.off[:, 0:4]), 0.25, None, mult, None, [r("iot"), r("off")], [r("ri")])
+        as_list("kr", "kw", 0.5, 31.5)
+        cp(T.cr[:, 16:272], T.ri[:, 0:64].indirect(T.kw[:, 0:16]), [r("ri"), r("kw")], [r("cr", 16, 272)])
+        as_list("cr", "cw", 1.0, 0.0)
+        if t == 0:
+            fill("ht", 256, 512, 0.0)
+            quant("hq0", "hs0", "zero", 128, 128)
+        for b in range(4):
+            mm(b, "pw", 128, "wq", "wp", 128 * b, "zc%d" % t, "zp%d" % t, 64)
+        for b in range(4):
+            act(T.ht[:, b:256:4], T.pw[:, 512 * b + 64:512 * b + 128], F.Relu, [bank("pw", b)], [("ht", 64 * b, 64 * b + 64)], scale=0.03125)
+        quant("hq%d" % t, "hs%d" % t, "ht", 0, 128)
+        send("h", t, frm)
+        arrival("h", t, to)
+        if t < R - 1:
+            ts(T.rm[:, 0:64], T.ri[:, 0:64], 3, None, AluOpType.bitwise_and, None, [r("ri")], [r("rm")])
+            ts(T.rm4[:, 0:64], T.rm[:, 0:64], 4.0, None, mult, None, [r("rm")], [r("rm4")])
+            cp(T.cm4[:, 0:256], T.rm4[:, 0:64].indirect(T.kw[:, 0:16]), [r("rm4"), r("kw")], [r("cm4")])
+            prekeys()
+            if t == 0:
+                quant("hc0", "hp0", "zero", 0, 128)
+            pads(t + 1)
+        else:
+            cp(T.cf[:, 0:256], T.cr[:, 16:272], [r("cr", 16, 272)], [r("cf")])
+            dma("y", "dol", T.ol[:], T.cf[0:128:16, 0:256], [r("cf")], [])
+            quant("qv", "sv", "vt", 0, 128)
+        new = "t%d" % (t + 1)
+        for b in (2, 0, 3, 1):
+            mm(b, "pw", 128, "eq", "esc", 128 * b, "hc%d" % t, "hp%d" % t, 64)
+        for b in (2, 3):
+            act(T.dh[:, 64 * b:64 * b + 64], T.pw[:, 512 * b + 64:512 * b + 128], F.Copy, [bank("pw", b)], [r("dh", 64 * b, 64 * b + 64)])
+            act(T.g2[:, C * (b - 2):C * (b - 1)], T.dh[:, 64 * b:64 * b + 64].indirect(T.cw[:, 0:16]), F.Copy,
+                [r("dh", 64 * b, 64 * b + 64), r("cw")], [r("g2", C * (b - 2), C * (b - 1))])
+        for b in (0, 1):
+            cp(T.dh[:, 64 * b:64 * b + 64], T.pw[:, 512 * b + 64:512 * b + 128], [bank("pw", b)], [r("dh", 64 * b, 64 * b + 64)])
+            tt(T[new][:, b:1024:4], T.dh[:, 64 * b:64 * b + 64].indirect(T.cw[:, 0:16]), T.fs[:, C * b:C * b + C], add,
+               [r("dh", 64 * b, 64 * b + 64), r("cw"), r("fs", C * b, C * b + C)], [(new, C * b, C * b + C)])
+        for h in range(2):
+            for b in (2, 3):
+                o, p, w = C * (b - 2) + 128 * h, 512 * b + 128 * h, C * b + 128 * h
+                tt(T[new][:, 512 * h + b:512 * h + 512:4], T.g2[:, o:o + 128], T.pf[:, p:p + 128], add,
+                   [r("g2", o, o + 128), bank("pf", b)], [(new, w, w + 128)])
+            quant("q%d" % (t + 1), "s%d" % (t + 1), new, 128 * h, 128, 128 * h)
+
+    for h in range(2):
+        mm(h, "pw", 128, "qv", "sv", 0, "q3", "s3", 128 * h)
+    dma("y", "doc", T.oc[:, 0:1024], T.q3[:, 0:256].bitcast(dt.uint8), [r("q3")], [])
+    for k in range(4):
+        dma("y", "ds%d" % k, T.osc[4 * k:4 * k + 4, 0:256], T.s3[32 * k:32 * k + 4, 0:256], [r("s3")], [])
+    cp(T.yo[:, 0:128], T.pw[:, 0:128], [bank("pw", 0)], [r("yo", 0, 128)])
+    act(T.yo[:, 128:256], T.pw[:, 512:640], F.Copy, [bank("pw", 1)], [r("yo", 128, 256)])
+    dma("s", "dy0", T.y[:, 0:128], T.yo[:, 0:128], [r("yo", 0, 128)], [])
+    dma("s", "dy1", T.y[:, 128:256], T.yo[:, 128:256], [r("yo", 128, 256)], [])
+    for sname in ("cv", "cs", "ct", "cg", "left"):
+        g.sync.wait_ge(T.sem[sname], count[sname])
+    for sname in DMAS:
+        if known["y"].get(sname, 0) < 16:
+            g.sync.wait_ge(T.sem[sname], 16)

@@ -1,4 +1,3 @@
-from concourse.bass import DstId, RemoteDMATransfer
 from concourse.mybir import dt, AluOpType, AxisListType, ActivationFunctionType
 
 C, K, R = 256, 64, 3
@@ -6,40 +5,21 @@ STEP = [1, 2, 4]
 PL = C + K
 CODES = "float8_e4m3fn_x4"
 
-SCRATCH = {
-    "ones": ("sbuf", [128, 516], "bfloat16"), "strip": ("sbuf", [128, 516], "bfloat16"), "zero": ("sbuf", [128, 512], "bfloat16"),
-    "eq": ("sbuf", [128, 512], CODES), "esc": ("sbuf", [128, 512], "uint8"),
-    "ut": ("sbuf", [128, 512], "bfloat16"), "qu": ("sbuf", [128, 128], CODES), "su": ("sbuf", [128, 128], "uint8"),
-    "uu": ("sbuf", [128, 256], CODES), "us": ("sbuf", [128, 256], "uint8"),
-    "vt": ("sbuf", [128, 512], "bfloat16"), "qv": ("sbuf", [128, 128], CODES), "sv": ("sbuf", [128, 128], "uint8"),
-    "wq": ("sbuf", [128, 512], CODES), "wp": ("sbuf", [128, 512], "uint8"),
-    "nxi": ("sbuf", [128, 16], "int32"), "coi": ("sbuf", [128, 16], "int32"),
-    "nxo": ("sbuf", [128, 16], "uint16"), "coo": ("sbuf", [128, 16], "uint16"),
-    "uoi": ("sbuf", [128, 16], "int32"), "uoo": ("sbuf", [128, 16], "uint16"),
-    "iot": ("sbuf", [128, 320], "float32"), "mi": ("sbuf", [128, 64], "int32"), "mi3": ("sbuf", [128, 64], "int32"),
-    "m4t": ("sbuf", [128, 64], "bfloat16"),
-    "pi": ("sbuf", [128, 4], "int32"), "p15": ("sbuf", [128, 4], "int32"), "p16": ("sbuf", [128, 4], "int32"),
-    "si": ("sbuf", [128, 4], "int32"), "kap": ("sbuf", [128, 4], "float32"), "kv": ("sbuf", [128, 4], "float32"),
-    "lo": ("sbuf", [128, 1], "float32"), "hi": ("sbuf", [128, 1], "float32"),
-    "flr": ("sbuf", [128, 272], "bfloat16"),
-    "fh": ("sbuf", [128, 4 * PL], "bfloat16"), "fs": ("sbuf", [128, 512], "bfloat16"),
-    "sa": ("sbuf", [128, 256], "bfloat16"), "sb": ("sbuf", [128, 256], "bfloat16"), "k1": ("sbuf", [128, 256], "bfloat16"),
-    "pk": ("sbuf", [128, 256], "bfloat16"), "cm4": ("sbuf", [128, 256], "bfloat16"), "cm16": ("sbuf", [128, 256], "bfloat16"),
-    "kr": ("sbuf", [128, 288], "bfloat16"), "cr": ("sbuf", [128, 288], "bfloat16"),
-    "ta": ("sbuf", [128, 256], "bfloat16"), "tb": ("sbuf", [128, 288], "bfloat16"),
-    "e1": ("sbuf", [128, 32], "float32"), "kwf": ("sbuf", [128, 16], "float32"),
-    "kw": ("sbuf", [128, 16], "uint16"), "cw": ("sbuf", [128, 16], "uint16"),
-    "junk": ("sbuf", [128, 4 * 272], "bfloat16"), "jun2": ("sbuf", [128, 256], "float32"),
-    "vv": ("sbuf", [128, 4], "float32"), "acc": ("sbuf", [128, 4], "float32"), "fr": ("sbuf", [128, 64], "float32"),
-    "f16": ("sbuf", [128, 4], "uint16"), "s16": ("sbuf", [128, 4], "uint16"), "off": ("sbuf", [128, 16], "uint16"),
-    "fi": ("sbuf", [128, 4], "int32"), "sd": ("sbuf", [128, 24], "float32"),
-    "g1": ("sbuf", [128, 256], "bfloat16"), "zk": ("sbuf", [128, 256], "bfloat16"),
-    "zt": ("sbuf", [128, 512], "bfloat16"), "ht": ("sbuf", [128, 512], "bfloat16"),
-    "ri": ("sbuf", [128, 64], "int32"), "rm": ("sbuf", [128, 64], "int32"), "rm4": ("sbuf", [128, 64], "bfloat16"),
-    "dh": ("sbuf", [128, 256], "bfloat16"), "g2": ("sbuf", [128, 512], "bfloat16"),
-    "cf": ("sbuf", [128, 256], "float32"), "yo": ("sbuf", [128, 256], "float32"),
-    "pf": ("psum", [128, 2048], "float32"), "pw": ("psum", [128, 2048], "float32"),
-}
+SCRATCH = {}
+for _n, _w, _d in (
+        ("ones", 516, "b"), ("strip", 516, "b"), ("zero", 512, "b"), ("eq", 512, "c"), ("esc", 512, "p"), ("ut", 512, "b"), ("qu", 128, "c"),
+        ("su", 128, "p"), ("uu", 256, "c"), ("us", 256, "p"), ("vt", 512, "b"), ("qv", 128, "c"), ("sv", 128, "p"), ("wq", 512, "c"), ("wp", 512, "p"),
+        ("nxi", 16, "i"), ("coi", 16, "i"), ("nxo", 16, "u"), ("coo", 16, "u"), ("uoi", 16, "i"), ("uoo", 16, "u"), ("iot", 320, "f"), ("mi", 64, "i"),
+        ("mi3", 64, "i"), ("m4t", 64, "b"), ("pi", 4, "i"), ("p15", 4, "i"), ("p16", 4, "i"), ("si", 4, "i"), ("kap", 4, "f"), ("kv", 4, "f"),
+        ("lo", 1, "f"), ("hi", 1, "f"), ("flr", 272, "b"), ("fh", 4 * PL, "b"), ("fs", 512, "b"), ("sa", 256, "b"), ("sb", 256, "b"), ("k1", 256, "b"),
+        ("pk", 256, "b"), ("cm4", 256, "b"), ("cm16", 256, "b"), ("kr", 288, "b"), ("cr", 288, "b"), ("ta", 256, "b"), ("tb", 288, "b"), ("e1", 32, "f"),
+        ("kwf", 16, "f"), ("kw", 16, "u"), ("cw", 16, "u"), ("junk", 1088, "b"), ("jun2", 256, "f"), ("vv", 4, "f"), ("acc", 4, "f"), ("fr", 64, "f"),
+        ("f16", 4, "u"), ("s16", 4, "u"), ("r16", 4, "u"), ("o16", 4, "u"), ("fi", 4, "i"), ("si2", 20, "i"), ("rr", 64, "b"), ("om", 256, "b"),
+        ("ow", 256, "b"), ("g1", 256, "b"), ("zk", 256, "b"), ("zt", 512, "b"), ("ht", 512, "b"), ("ri", 64, "i"), ("rm", 64, "i"), ("rm4", 64, "b"),
+        ("dh", 256, "b"), ("g2", 512, "b"), ("cf", 256, "f"), ("yo", 256, "f")):
+    SCRATCH[_n] = ("sbuf", [128, _w], {"b": "bfloat16", "c": CODES, "p": "uint8", "i": "int32", "u": "uint16", "f": "float32"}[_d])
+for _n in ("pf", "pw"):
+    SCRATCH[_n] = ("psum", [128, 2048], "float32")
 for _i in range(4):
     SCRATCH["m%d" % _i] = ("sbuf", [128, 272], "bfloat16")
     SCRATCH["w%d" % _i] = ("sbuf", [128, 272], "bfloat16")
@@ -48,12 +28,12 @@ for _i in range(4):
     SCRATCH["s%d" % _i] = ("sbuf", [128, 256], "uint8")
 for _i in range(R):
     for _n in "zh":
-        SCRATCH["%sq%d" % (_n, _i)] = ("sbuf", [128, 256], CODES)
-        SCRATCH["%ss%d" % (_n, _i)] = ("sbuf", [128, 256], "uint8")
+        SCRATCH["%sq%d" % (_n, _i)] = ("sbuf", [128, 128], CODES)
+        SCRATCH["%ss%d" % (_n, _i)] = ("sbuf", [128, 128], "uint8")
         SCRATCH["%sc%d" % (_n, _i)] = ("sbuf", [128, 192], CODES)
-        SCRATCH["%sp%d" % (_n, _i)] = ("sbuf", [128, 384], "uint8")
+        SCRATCH["%sp%d" % (_n, _i)] = ("sbuf", [128, 192], "uint8")
 
-DMAS = ["dx", "du", "dv", "dwc", "dws", "dn", "dc", "dol", "dy0", "dy1", "doc", "ds0", "ds1", "ds2", "ds3"]
+DMAS = ["dx0", "dx1", "du", "dv", "dwc", "dws", "dn", "dc", "dol", "dy0", "dy1", "doc0", "doc1", "ds0", "ds1", "ds2", "ds3"]
 SEMAPHORES = ["cv", "cs", "ct", "cg", "left"] + ["za%d" % i for i in range(R)] + ["ha%d" % i for i in range(R)] + DMAS
 
 
@@ -61,7 +41,7 @@ def rank_program(g, core, T, topo):
     rank = T.rank_of(core)
     if rank is None:
         return
-    add, sub, mult, amax = AluOpType.add, AluOpType.subtract, AluOpType.mult, AluOpType.max
+    add, mult, amax = AluOpType.add, AluOpType.mult, AluOpType.max
     F = ActivationFunctionType
     eng = {"v": g.vector, "s": g.scalar, "t": g.tensor, "g": g, "y": g.sync}
     count = {"cv": 0, "cs": 0, "ct": 0, "cg": 0, "left": 0}
@@ -119,9 +99,14 @@ def rank_program(g, core, T, topo):
         return (name, a, T[name].shape[1] if b is None else b)
 
     def quant(qb, sb_, tile, a, n, c0=0):
+        if tile == "t0":
+            src = [(tile, 4 * c0, 4 * (c0 + n))]
+        elif tile in ("t1", "t2", "t3"):
+            src = [(tile, C * b + c0, C * b + c0 + n) for b in range(4)]
+        else:
+            src = [r(tile)]
         op("v", lambda: V.quantize_mx(T[qb][:, a:a + n], T[sb_][:, a:a + n], T[tile][:, 4 * c0:4 * (c0 + n)]),
-           [(tile, C * b + c0, C * b + c0 + n) for b in range(4)] if tile in ("t1", "t2", "t3") else [r(tile)],
-           [r(qb, a, a + n), r(sb_, a, a + n)])
+           src, [r(qb, a, a + n), r(sb_, a, a + n)])
 
     def fill(name, a, b, val):
         op("v", lambda: V.memset(T[name][:, a:b], val), [], [r(name, a, b)])
@@ -151,26 +136,20 @@ def rank_program(g, core, T, topo):
 
     def send(kind, t, peer):
         cq, sq = kind + "q%d" % t, kind + "s%d" % t
-        need("g", [r(cq, 0, 64), r(sq)], [])
+        need("g", [r(cq, 0, 64), r(sq, 0, 64)], [])
         dst = T.cores[peer]
         rid, pid, _se = topo.addr(dst)
-        e = topo.engines(core, dst)
-        half = len(e) // 2
-        arr = T.sem[kind + "a%d" % t]
-        tr = [RemoteDMATransfer(dst_ids=[DstId(rid=rid, pnc=pid)], dma_engine_mask=sum(1 << k for k in e[:half]), remote_sem=arr,
-                                src=T[cq][:, 0:64].bitcast(dt.uint8), dst=T[kind + "c%d" % t][:, 128:192].bitcast(dt.uint8)),
-              RemoteDMATransfer(dst_ids=[DstId(rid=rid, pnc=pid)], dma_engine_mask=sum(1 << k for k in e[half:]), remote_sem=arr,
-                                src=T[sq][:, 0:256], dst=T[kind + "p%d" % t][:, 128:384])]
-        g.remote_dma_fused(tr, local_sem=T.sem.left)
-        count["left"] += len(e)
+        m, arr = topo.mask(core, dst), T.sem[kind + "a%d" % t]
+        g.remote_dma(T[kind + "c%d" % t][:, 128:192].bitcast(dt.uint8), T[cq][:, 0:64].bitcast(dt.uint8), arr, T.sem.left, pid, rid, m)
+        g.remote_dma(T[kind + "p%d" % t][:, 128:192], T[sq][:, 0:64], arr, T.sem.left, pid, rid, m)
+        count["left"] += 2 * len(topo.engines(core, dst))
 
     def arrival(kind, t, peer):
-        n = len(topo.engines(T.cores[peer], core))
-        note("r", [], [(kind + "c%d" % t, 128, 192), (kind + "p%d" % t, 128, 384)], kind + "a%d" % t, n)
+        n = 2 * len(topo.engines(T.cores[peer], core))
+        note("r", [], [(kind + "c%d" % t, 128, 192), (kind + "p%d" % t, 128, 192)], kind + "a%d" % t, n)
 
     def pads(t):
         for k in "zh":
-            quant(k + "q%d" % t, k + "s%d" % t, "zero", 128, 128)
             quant(k + "c%d" % t, k + "p%d" % t, "zero", 0, 128)
 
     def as_list(row, dest, scale, base):
@@ -183,44 +162,45 @@ def rank_program(g, core, T, topo):
         tt(T.kwf[:, 1:16:2], T.e1[:, 8:16], T.e1[:, 24:32], add, [r("e1", 8, 16), r("e1", 24, 32)], [("kwf", 8, 16)])
         ts(T[dest][:, 0:16], T.kwf[:, 0:16], scale, base, mult, add, [r("kwf")], [r(dest)])
 
-    def prekeys():
-        ts(T.cm16[:, 0:256], T.cm4[:, 0:256], 4.0, 2.0, mult, add, [r("cm4")], [r("cm16")])
+    def prekeys(first):
+        if first:
+            act(T.cm16[:, 0:256], T.cm4[:, 0:256], F.Copy, [r("cm4")], [r("cm16")], bias=2.0, scale=4.0)
+        else:
+            ts(T.cm16[:, 0:256], T.cm4[:, 0:256], 4.0, 2.0, mult, add, [r("cm4")], [r("cm16")])
         tt(T.pk[:, 0:256], T.cm4[:, 0:256].indirect(T.nxo[:, 0:16]), T.cm16[:, 0:256], add, [r("cm4"), r("nxo"), r("cm16")], [r("pk")])
 
-    dma("y", "dx", T.t0[:], T.x[:], [], [r("t0")])
+    dma("y", "du", T.ut[:], T.u[:], [], [r("ut")])
+    for h in range(2):
+        dma("y", "dx%d" % h, T.t0[:, 512 * h:512 * h + 512], T.x[:, 512 * h:512 * h + 512], [], [r("t0", 512 * h, 512 * h + 512)])
     dma("s", "dc", T.coi[:], T.co[:], [], [r("coi")])
     dma("s", "dn", T.nxi[:], T.nx[:], [], [r("nxi")])
-    dma("s", "du", T.ut[:], T.u[:], [], [r("ut")])
     fill("ones", 0, 516, 1.0)
     op("g", lambda: g.iota(T.mi[:, 0:64], [[1, 64]], 0, 0), [], [r("mi")])
+    op("g", lambda: g.affine_select(T.strip[:, 0:516], T.ones[:, 0:516], [[-1, 516]], AluOpType.is_equal, 0.0, 3, 4), [r("ones")], [r("strip")])
     op("g", lambda: g.iota(T.pi[:, 0:4], [[0, 4]], 0, 1), [], [r("pi")])
     op("g", lambda: g.iota(T.si[:, 0:4], [[16, 4]], 0, 0), [], [r("si")])
-    op("g", lambda: g.affine_select(T.strip[:, 0:516], T.ones[:, 0:516], [[-1, 516]], AluOpType.is_equal, 0.0, 3, 4), [r("ones")], [r("strip")])
     op("g", lambda: g.iota(T.uoi[:, 0:16], [[1, 2], [16, 8]], 0, 0), [], [r("uoi")])
     op("g", lambda: g.iota(T.iot[:, 0:320], [[1, 320]], 0, 0, allow_small_or_imprecise_dtypes=True), [], [r("iot")])
-    fill("zero", 0, 512, 0.0)
     ts(T.mi3[:, 0:64], T.mi[:, 0:64], 3, None, AluOpType.bitwise_and, None, [r("mi")], [r("mi3")])
     ts(T.m4t[:, 0:64], T.mi3[:, 0:64], 4.0, None, mult, None, [r("mi3")], [r("m4t")])
-    ts(T.p15[:, 0:4], T.pi[:, 0:4], 15, None, AluOpType.bitwise_and, None, [r("pi")], [r("p15")])
-    tt(T.kap[:, 0:4], T.p15[:, 0:4], T.si[:, 0:4], add, [r("p15"), r("si")], [r("kap")])
-    ts(T.kv[:, 0:4], T.kap[:, 0:4], 2.0, -63.0, mult, add, [r("kap")], [r("kv")])
     for i in range(4):
-        cp(T["m%d" % i][:, 256:257], T.kap[:, i:i + 1], [r("kap")], [r("m%d" % i, 256, 257)])
-        fill("w%d" % i, 257, 258, 0.0625)
+        fill("w%d" % i, 257, 258, 0.1875)
         fill("fh", PL * i + C, PL * i + PL, 0.0)
-    fill("flr", 0, 272, 2.0 ** -20)
-    fill("zt", 256, 512, 0.0)
-    cp(T.coo[:, 0:16], T.coi[:, 0:16], [r("coi")], [r("coo")])
-    cp(T.nxo[:, 0:16], T.nxi[:, 0:16], [r("nxi")], [r("nxo")])
-    act(T.cm4[:, 0:256], T.m4t[:, 0:64].indirect(T.coo[:, 0:16]), F.Copy, [r("m4t"), r("coo")], [r("cm4")])
+    fill("flr", 0, 256, 2.0 ** -20)
+    fill("flr", 256, 257, 0.0625)
     for b in range(4):
         op("v", lambda: V.quantize_mx(T.eq[:, 128 * b:128 * b + 128], T.esc[:, 128 * b:128 * b + 128], T.strip[:, 3 - b:515 - b]),
            [r("strip")], [r("eq", 128 * b, 128 * b + 128), r("esc", 128 * b, 128 * b + 128)])
+    cp(T.coo[:, 0:16], T.coi[:, 0:16], [r("coi")], [r("coo")])
+    cp(T.nxo[:, 0:16], T.nxi[:, 0:16], [r("nxi")], [r("nxo")])
+    act(T.cm4[:, 0:256], T.m4t[:, 0:64].indirect(T.coo[:, 0:16]), F.Copy, [r("m4t"), r("coo")], [r("cm4")])
+    ts(T.p15[:, 0:4], T.pi[:, 0:4], 15, None, AluOpType.bitwise_and, None, [r("pi")], [r("p15")])
     cp(T.uoo[:, 0:16], T.uoi[:, 0:16], [r("uoi")], [r("uoo")])
-    quant("zq0", "zs0", "zero", 128, 128)
-    prekeys()
+    tt(T.kap[:, 0:4], T.p15[:, 0:4], T.si[:, 0:4], add, [r("p15"), r("si")], [r("kap")])
     quant("qu", "su", "ut", 0, 128)
+    ts(T.kv[:, 0:4], T.kap[:, 0:4], 2.0, -63.0, mult, add, [r("kap")], [r("kv")])
     cp(T.uu[:, 0:256].bitcast(dt.uint32), T.qu[:, 0:128].bitcast(dt.uint32).indirect(T.uoo[:, 0:16]), [r("qu"), r("uoo")], [r("uu")])
+    prekeys(True)
     act(T.us[:, 0:256], T.su[:, 0:128].indirect(T.uoo[:, 0:16]), F.Copy, [r("su"), r("uoo")], [r("us")])
     need("y", [r("t0")], [])
     dma("y", "dwc", T.wq[:, 0:512].bitcast(dt.uint8), T.wc[:, 0:2048], [], [r("wq")])
@@ -228,6 +208,8 @@ def rank_program(g, core, T, topo):
     dma("y", "dv", T.vt[:], T.v[:], [], [r("vt")])
     for h in range(2):
         quant("q0", "s0", "t0", 128 * h, 128, 128 * h)
+    for i in range(4):
+        cp(T["m%d" % i][:, 256:257], T.kap[:, i:i + 1], [r("kap")], [r("m%d" % i, 256, 257)])
 
     for t in range(R):
         q, s = "q%d" % t, "s%d" % t
@@ -237,12 +219,13 @@ def rank_program(g, core, T, topo):
                 mm(2 * h + k, "pw", 128, "uu", "us", 128 * k, q, s, 128 * h)
         for b in range(4):
             mm(b, "pf", 256, "eq", "esc", 128 * b, q, s, 0)
-        for h in range(2):
-            a, e = 128 * h, 128 * h + 128
-            for k, n in enumerate(("sa", "sb")):
-                act(T[n][:, a:e], T.pw[:, 1024 * h + 512 * k:1024 * h + 512 * k + 128], F.Sign, [bank("pw", 2 * h + k)], [r(n, a, e)],
-                    bias=-1e-36, scale=-1.0)
+        for h, k in ((0, 0), (0, 1), (1, 0), (1, 1)):
+            n, a, e = ("sa", "sb")[k], 128 * h, 128 * h + 128
+            act(T[n][:, a:e], T.pw[:, 1024 * h + 512 * k:1024 * h + 512 * k + 128], F.Sign, [bank("pw", 2 * h + k)], [r(n, a, e)],
+                bias=-1e-36, scale=-1.0)
+        for a, e in ((0, 128), (128, 256)):
             tt(T.k1[:, a:e], T.sa[:, a:e], T.pk[:, a:e], add, [r("sa", a, e), r("pk", a, e)], [r("k1", a, e)])
+        for a, e in ((0, 128), (128, 256)):
             tt(T.kr[:, 16 + a:16 + e], T.k1[:, a:e], T.sb[:, a:e], mult, [r("k1", a, e), r("sb", a, e)], [r("kr", 16 + a, 16 + e)])
 
         def half_f(b):
@@ -254,46 +237,73 @@ def rank_program(g, core, T, topo):
 
         def scan(i):
             op("v", lambda: V.tensor_tensor_scan(T["w%d" % i][:, 0:257], T["m%d" % i][:, 0:257], T.flr[:, 0:257], 1.0, mult, amax),
-               [r("m%d" % i, 0, 257), r("flr")], [r("w%d" % i, 0, 257)])
-            if i < 3:
+               [r("m%d" % i, 0, 257), r("flr", 0, 257)], [r("w%d" % i, 0, 257)])
+
+        def total(i):
+            if i != 2:
                 act(T.junk[:, 272 * i:272 * i + 258], T["w%d" % i][:, 0:258], F.Copy, [r("w%d" % i, 0, 258)],
                     [r("junk", 272 * i, 272 * i + 272), r("vv", i, i + 1)], accum_out=T.vv[:, i:i + 1])
             else:
-                op("v", lambda: V.tensor_reduce(T.vv[:, 3:4], T.w3[:, 0:258], AxisListType.X, add), [r("w3", 0, 258)], [r("vv", 3, 4)])
+                op("v", lambda: V.tensor_reduce(T.vv[:, i:i + 1], T["w%d" % i][:, 0:258], AxisListType.X, add),
+                   [r("w%d" % i, 0, 258)], [r("vv", i, i + 1)])
         half_f(0)
         half_f(1)
         mask(0)
         mask(1)
         scan(0)
+        total(0)
         mask(2)
         scan(1)
+        total(1)
         mask(3)
         scan(2)
         scan(3)
+        total(3)
+        total(2)
         half_f(2)
-        half_f(3)
-        cp(T.f16[:, 0:4], T.vv[:, 0:4], [r("vv")], [r("f16")])
+        d = [T.si2[:, 4 * k:4 * k + 4] for k in range(5)]
+        e = [r("si2", 4 * k, 4 * k + 4) for k in range(5)]
+        ts(T.f16[:, 0:4], T.vv[:, 0:4], -0.1875, None, add, None, [r("vv")], [r("f16")])
+        ts(d[0], T.vv[:, 0:4], 1024.0, None, mult, None, [r("vv")], [e[0]])
         cp(T.fr[:, 0:64], T.iot[:, 0:320].indirect(T.f16[:, 0:4]), [r("iot"), r("f16")], [r("fr")])
         for i in range(4):
             act(T.jun2[:, 64 * i:64 * i + 64], T.fr[:, 0:64], F.Sign, [r("fr"), r("vv")], [r("jun2", 64 * i, 64 * i + 64), r("acc", i, i + 1)],
                 bias=T.vv[:, i:i + 1], scale=-1.0, accum_out=T.acc[:, i:i + 1])
         for b in range(4):
+            if b == 2:
+                half_f(3)
             act(T.g1[:, 64 * b:64 * b + 64], T.fh[:, PL * b:PL * b + PL].indirect(T.f16[:, 0:4]), F.Copy,
                 [r("fh", PL * b, PL * b + PL), r("f16")], [r("g1", 64 * b, 64 * b + 64)])
-        cp(T.fi[:, 0:4], T.vv[:, 0:4], [r("vv")], [r("fi")])
-        tt(T.sd[:, 0:4], T.vv[:, 0:4], T.fi[:, 0:4], sub, [r("vv"), r("fi")], [r("sd", 0, 4)])
-        ts(T.sd[:, 4:8], T.sd[:, 0:4], 1024.0, -63.875, mult, add, [r("sd", 0, 4)], [r("sd", 4, 8)])
-        tt(T.sd[:, 8:12], T.sd[:, 4:8], T.fi[:, 0:4], add, [r("sd", 4, 8), r("fi")], [r("sd", 8, 12)])
-        ts(T.sd[:, 12:16], T.sd[:, 8:12], 255.7, None, AluOpType.is_lt, None, [r("sd", 8, 12)], [r("sd", 12, 16)])
-        tt(T.sd[:, 16:20], T.sd[:, 12:16], T.sd[:, 4:8], mult, [r("sd", 4, 8), r("sd", 12, 16)], [r("sd", 16, 20)])
-        tt(T.sd[:, 20:24], T.sd[:, 16:20], T.fi[:, 0:4], add, [r("sd", 16, 20), r("fi")], [r("sd", 20, 24)])
-        cp(T.s16[:, 0:4], T.sd[:, 20:24], [r("sd", 20, 24)], [r("s16")])
-        for b in range(4):
-            ts(T.off[:, 4 * b:4 * b + 4], T.acc[:, 0:4], 2.0, 124.0 + b, mult, add, [r("acc")], [r("off", 4 * b, 4 * b + 4)])
-        for b in range(4):
+
+        def mean(b):
             tt(T.zk[:, 64 * b:64 * b + 64], T.fh[:, PL * b:PL * b + PL].indirect(T.s16[:, 0:4]), T.g1[:, 64 * b:64 * b + 64], add,
                [r("fh", PL * b, PL * b + PL), r("s16"), r("g1", 64 * b, 64 * b + 64)], [r("zk", 64 * b, 64 * b + 64)])
-        cp(T.zt[:, 0:256].indirect(T.off[:, 0:16]), T.zk[:, 0:256], [r("zk"), r("off")], [r("zt", 0, 256)])
+        ts(T.fi[:, 0:4], d[0], 10, None, AluOpType.arith_shift_right, None, [e[0]], [r("fi")])
+        ts(d[1], d[0], 1023, None, AluOpType.bitwise_and, None, [e[0]], [e[1]])
+        tt(d[2], T.fi[:, 0:4], d[1], add, [r("fi"), e[1]], [e[2]])
+        ts(d[3], d[2], 255, None, AluOpType.bitwise_and, None, [e[2]], [e[3]])
+        tt(d[4], d[3], T.fi[:, 0:4], amax, [e[3], r("fi")], [e[4]])
+        ts(T.r16[:, 0:4], T.acc[:, 0:4], 0.5, 31.0, mult, add, [r("acc")], [r("r16")])
+        cp(T.s16[:, 0:4], d[4], [e[4]], [r("s16")])
+        cp(T.rr[:, 0:64], T.iot[:, 0:320].indirect(T.r16[:, 0:4]), [r("iot"), r("r16")], [r("rr")])
+        mean(0)
+        for i in range(4):
+            ts(T.om[:, 64 * i:64 * i + 64], T.rr[:, 0:64], T.kap[:, i:i + 1], None, AluOpType.not_equal, None,
+               [r("rr"), r("kap")], [r("om", 64 * i, 64 * i + 64)])
+        mean(1)
+        op("v", lambda: V.tensor_tensor_scan(T.ow[:, 0:256], T.ones[:, 0:256], T.om[:, 0:256], 0.0, add, mult), [r("ones"), r("om")], [r("ow")])
+        mean(2)
+        ts(T.o16[:, 0:4], T.ow[:, 63:256:64], -1.0, 63.0, mult, add, [r("ow")], [r("o16")])
+        mean(3)
+        for b in range(4):
+            o, i, rd, wr = T.zt[:, b:256:4], T.zk[:, 64 * b:64 * b + 64].indirect(T.o16[:, 0:4]), \
+                [r("zk", 64 * b, 64 * b + 64), r("o16")], [("zt", 64 * b, 64 * b + 64)]
+            if b < 2:
+                act(o, i, F.Copy, rd, wr)
+            else:
+                cp(o, i, rd, wr)
+        if t == 0:
+            fill("zt", 256, 512, 0.0)
         quant("zq%d" % t, "zs%d" % t, "zt", 0, 128)
         send("z", t, to)
         arrival("z", t, frm)
@@ -306,14 +316,12 @@ def rank_program(g, core, T, topo):
             for n in ("kr", "cr"):
                 fill(n, 0, 16, 0.0)
                 fill(n, 272, 288, 0.0)
-            quant("zc0", "zp0", "zero", 0, 128)
-        ts(T.ri[:, 0:64], T.iot[:, 0:320].indirect(T.off[:, 0:4]), 0.25, None, mult, None, [r("iot"), r("off")], [r("ri")])
-        as_list("kr", "kw", 0.5, 31.5)
-        cp(T.cr[:, 16:272], T.ri[:, 0:64].indirect(T.kw[:, 0:16]), [r("ri"), r("kw")], [r("cr", 16, 272)])
-        as_list("cr", "cw", 1.0, 0.0)
-        if t == 0:
+            fill("zero", 0, 512, 0.0)
             fill("ht", 256, 512, 0.0)
-            quant("hq0", "hs0", "zero", 128, 128)
+            pads(0)
+        as_list("kr", "kw", 0.5, 31.5)
+        cp(T.cr[:, 16:272], T.rr[:, 0:64].indirect(T.kw[:, 0:16]), [r("rr"), r("kw")], [r("cr", 16, 272)])
+        as_list("cr", "cw", 1.0, 0.0)
         for b in range(4):
             mm(b, "pw", 128, "wq", "wp", 128 * b, "zc%d" % t, "zp%d" % t, 64)
         for b in range(4):
@@ -322,24 +330,29 @@ def rank_program(g, core, T, topo):
         send("h", t, frm)
         arrival("h", t, to)
         if t < R - 1:
+            cp(T.ri[:, 0:64], T.rr[:, 0:64], [r("rr")], [r("ri")])
             ts(T.rm[:, 0:64], T.ri[:, 0:64], 3, None, AluOpType.bitwise_and, None, [r("ri")], [r("rm")])
             ts(T.rm4[:, 0:64], T.rm[:, 0:64], 4.0, None, mult, None, [r("rm")], [r("rm4")])
             cp(T.cm4[:, 0:256], T.rm4[:, 0:64].indirect(T.kw[:, 0:16]), [r("rm4"), r("kw")], [r("cm4")])
-            prekeys()
-            if t == 0:
-                quant("hc0", "hp0", "zero", 0, 128)
+            prekeys(False)
             pads(t + 1)
         else:
             cp(T.cf[:, 0:256], T.cr[:, 16:272], [r("cr", 16, 272)], [r("cf")])
             dma("y", "dol", T.ol[:], T.cf[0:128:16, 0:256], [r("cf")], [])
             quant("qv", "sv", "vt", 0, 128)
         new = "t%d" % (t + 1)
-        for b in (2, 0, 3, 1):
+        for b in (0, 2, 3, 1):
             mm(b, "pw", 128, "eq", "esc", 128 * b, "hc%d" % t, "hp%d" % t, 64)
+
+        def gather(b, h):
+            o = C * (b - 2) + 128 * h
+            act(T.g2[:, o:o + 128], T.dh[:, 64 * b:64 * b + 64].indirect(T.cw[:, 8 * h:8 * h + 8]), F.Copy,
+                [r("dh", 64 * b, 64 * b + 64), r("cw")], [r("g2", o, o + 128)])
         for b in (2, 3):
             act(T.dh[:, 64 * b:64 * b + 64], T.pw[:, 512 * b + 64:512 * b + 128], F.Copy, [bank("pw", b)], [r("dh", 64 * b, 64 * b + 64)])
-            act(T.g2[:, C * (b - 2):C * (b - 1)], T.dh[:, 64 * b:64 * b + 64].indirect(T.cw[:, 0:16]), F.Copy,
-                [r("dh", 64 * b, 64 * b + 64), r("cw")], [r("g2", C * (b - 2), C * (b - 1))])
+            gather(b, 0)
+        gather(2, 1)
+        gather(3, 1)
         for b in (0, 1):
             cp(T.dh[:, 64 * b:64 * b + 64], T.pw[:, 512 * b + 64:512 * b + 128], [bank("pw", b)], [r("dh", 64 * b, 64 * b + 64)])
             tt(T[new][:, b:1024:4], T.dh[:, 64 * b:64 * b + 64].indirect(T.cw[:, 0:16]), T.fs[:, C * b:C * b + C], add,
@@ -352,14 +365,14 @@ def rank_program(g, core, T, topo):
             quant("q%d" % (t + 1), "s%d" % (t + 1), new, 128 * h, 128, 128 * h)
 
     for h in range(2):
+        dma("y", "doc%d" % h, T.oc[:, 512 * h:512 * h + 512], T.q3[:, 128 * h:128 * h + 128].bitcast(dt.uint8), [r("q3", 128 * h, 128 * h + 128)], [])
         mm(h, "pw", 128, "qv", "sv", 0, "q3", "s3", 128 * h)
-    dma("y", "doc", T.oc[:, 0:1024], T.q3[:, 0:256].bitcast(dt.uint8), [r("q3")], [])
+    act(T.yo[:, 0:128], T.pw[:, 0:128], F.Copy, [bank("pw", 0)], [r("yo", 0, 128)])
+    dma("s", "dy0", T.y[:, 0:128], T.yo[:, 0:128], [r("yo", 0, 128)], [])
+    cp(T.yo[:, 128:256], T.pw[:, 512:640], [bank("pw", 1)], [r("yo", 128, 256)])
+    dma("s", "dy1", T.y[:, 128:256], T.yo[:, 128:256], [r("yo", 128, 256)], [])
     for k in range(4):
         dma("y", "ds%d" % k, T.osc[4 * k:4 * k + 4, 0:256], T.s3[32 * k:32 * k + 4, 0:256], [r("s3")], [])
-    cp(T.yo[:, 0:128], T.pw[:, 0:128], [bank("pw", 0)], [r("yo", 0, 128)])
-    act(T.yo[:, 128:256], T.pw[:, 512:640], F.Copy, [bank("pw", 1)], [r("yo", 128, 256)])
-    dma("s", "dy0", T.y[:, 0:128], T.yo[:, 0:128], [r("yo", 0, 128)], [])
-    dma("s", "dy1", T.y[:, 128:256], T.yo[:, 128:256], [r("yo", 128, 256)], [])
     for sname in ("cv", "cs", "ct", "cg", "left"):
         g.sync.wait_ge(T.sem[sname], count[sname])
     for sname in DMAS:

@@ -2,27 +2,31 @@ from concourse.mybir import dt, AluOpType, AxisListType, ActivationFunctionType
 
 C, K, R = 256, 64, 3
 STEP = [1, 2, 4]
-PL = C + K
+PL = C + 16
+ZL = K + 16
+REV = (2, 3)
+HOR = 256
 CODES = "float8_e4m3fn_x4"
 
 SCRATCH = {}
 for _n, _w, _d in (
-        ("ones", 516, "b"), ("strip", 516, "b"), ("zero", 512, "b"), ("eq", 512, "c"), ("esc", 512, "p"), ("ut", 512, "b"), ("qu", 128, "c"),
+        ("ones", 512, "b"), ("strip", 516, "b"), ("zero", 512, "b"), ("eq", 512, "c"), ("esc", 512, "p"), ("ut", 512, "b"), ("qu", 128, "c"),
         ("su", 128, "p"), ("uu", 256, "c"), ("us", 256, "p"), ("vt", 512, "b"), ("qv", 128, "c"), ("sv", 128, "p"), ("wq", 512, "c"), ("wp", 512, "p"),
-        ("nxi", 16, "i"), ("coi", 16, "i"), ("nxo", 16, "u"), ("coo", 16, "u"), ("uoi", 16, "i"), ("uoo", 16, "u"), ("iot", 320, "f"), ("mi", 64, "i"),
-        ("mi3", 64, "i"), ("m4t", 64, "b"), ("pi", 4, "i"), ("p15", 4, "i"), ("p16", 4, "i"), ("si", 4, "i"), ("kap", 4, "f"), ("kv", 4, "f"),
-        ("lo", 1, "f"), ("hi", 1, "f"), ("flr", 272, "b"), ("fh", 4 * PL, "b"), ("fs", 512, "b"), ("sa", 256, "b"), ("sb", 256, "b"), ("k1", 256, "b"),
-        ("pk", 256, "b"), ("cm4", 256, "b"), ("cm16", 256, "b"), ("kr", 288, "b"), ("cr", 288, "b"), ("ta", 256, "b"), ("tb", 288, "b"), ("e1", 32, "f"),
-        ("kwf", 16, "f"), ("kw", 16, "u"), ("cw", 16, "u"), ("junk", 1088, "b"), ("jun2", 256, "f"), ("vv", 4, "f"), ("acc", 4, "f"), ("fr", 64, "f"),
-        ("f16", 4, "u"), ("s16", 4, "u"), ("r16", 4, "u"), ("o16", 4, "u"), ("fi", 4, "i"), ("si2", 20, "i"), ("rr", 64, "b"), ("om", 256, "b"),
-        ("ow", 256, "b"), ("g1", 256, "b"), ("zk", 256, "b"), ("zt", 512, "b"), ("ht", 512, "b"), ("ri", 64, "i"), ("rm", 64, "i"), ("rm4", 64, "b"),
-        ("dh", 256, "b"), ("g2", 512, "b"), ("cf", 256, "f"), ("yo", 256, "f")):
+        ("nxi", 16, "i"), ("coi", 16, "i"), ("nxo", 16, "u"), ("coo", 16, "u"), ("uoi", 16, "i"), ("uoo", 16, "u"), ("iot", 272, "f"), ("pif", 1, "f"),
+        ("m4t", 64, "b"), ("pi", 4, "i"), ("p15", 4, "i"), ("p16", 4, "i"), ("si", 4, "i"), ("kap", 4, "f"), ("kv", 4, "f"),
+        ("lo", 1, "f"), ("hi", 1, "f"), ("nka", 1, "f"), ("fh", 4 * PL, "b"), ("sa", 256, "b"), ("sb", 256, "b"),
+        ("k1", 256, "b"), ("pk", 256, "b"), ("cm4", 256, "b"), ("cm16", 256, "b"), ("kr", 288, "b"), ("cr", 288, "b"), ("ta", 256, "b"),
+        ("tb", 288, "b"), ("e1", 32, "f"), ("kwf", 16, "f"), ("kw", 16, "u"), ("cw", 16, "u"), ("junk", 512, "b"), ("jun2", 256, "f"),
+        ("ww", 1024, "f"), ("acc", 4, "f"), ("fr", 64, "f"), ("lt", 65, "b"), ("f16", 4, "u"), ("s16", 4, "u"), ("r16", 4, "u"), ("o16", 4, "u"),
+        ("fi", 4, "i"), ("si2", 20, "i"), ("rr", 64, "b"), ("om", 256, "b"), ("ow", 256, "b"), ("g1", 256, "b"), ("zk", 4 * ZL, "b"),
+        ("zt", 512, "b"), ("ht", 512, "b"), ("ri", 64, "i"), ("rm", 64, "i"), ("rm4", 64, "b"), ("dh", 256, "b"), ("g2", 512, "b"), ("cf", 256, "f"),
+        ("yo", 256, "f"), ("w0", 256, "b"), ("w1", 256, "b"),
+        ("zc", 128 + R * K, "c"), ("zp", 128 + R * K, "p"), ("hc", 128 + R * K, "c"), ("hp", 128 + R * K, "p")):
     SCRATCH[_n] = ("sbuf", [128, _w], {"b": "bfloat16", "c": CODES, "p": "uint8", "i": "int32", "u": "uint16", "f": "float32"}[_d])
 for _n in ("pf", "pw"):
     SCRATCH[_n] = ("psum", [128, 2048], "float32")
 for _i in range(4):
-    SCRATCH["m%d" % _i] = ("sbuf", [128, 272], "bfloat16")
-    SCRATCH["w%d" % _i] = ("sbuf", [128, 272], "bfloat16")
+    SCRATCH["m%d" % _i] = ("sbuf", [128, 256], "bfloat16")
     SCRATCH["t%d" % _i] = ("sbuf", [128, 1024], "bfloat16")
     SCRATCH["q%d" % _i] = ("sbuf", [128, 256], CODES)
     SCRATCH["s%d" % _i] = ("sbuf", [128, 256], "uint8")
@@ -30,8 +34,6 @@ for _i in range(R):
     for _n in "zh":
         SCRATCH["%sq%d" % (_n, _i)] = ("sbuf", [128, 128], CODES)
         SCRATCH["%ss%d" % (_n, _i)] = ("sbuf", [128, 128], "uint8")
-        SCRATCH["%sc%d" % (_n, _i)] = ("sbuf", [128, 192], CODES)
-        SCRATCH["%sp%d" % (_n, _i)] = ("sbuf", [128, 192], "uint8")
 
 DMAS = ["dx0", "dx1", "du", "dv", "dwc", "dws", "dn", "dc", "dol", "dy0", "dy1", "doc0", "doc1", "ds0", "ds1", "ds2", "ds3"]
 SEMAPHORES = ["cv", "cs", "ct", "cg", "left"] + ["za%d" % i for i in range(R)] + ["ha%d" % i for i in range(R)] + DMAS
@@ -111,6 +113,9 @@ def rank_program(g, core, T, topo):
     def fill(name, a, b, val):
         op("v", lambda: V.memset(T[name][:, a:b], val), [], [r(name, a, b)])
 
+    def whole(name, a, b, pattern, base=0, per=0):
+        op("g", lambda: g.iota(T[name][:, a:b], pattern, base, per, allow_small_or_imprecise_dtypes=True), [], [r(name, a, b)])
+
     def ts(out, in0, s1, s2, op0, op1, reads, writes):
         if s2 is None:
             op("v", lambda: V.tensor_scalar(out, in0, s1, None, op0), reads, writes)
@@ -140,17 +145,15 @@ def rank_program(g, core, T, topo):
         dst = T.cores[peer]
         rid, pid, _se = topo.addr(dst)
         m, arr = topo.mask(core, dst), T.sem[kind + "a%d" % t]
-        g.remote_dma(T[kind + "c%d" % t][:, 128:192].bitcast(dt.uint8), T[cq][:, 0:64].bitcast(dt.uint8), arr, T.sem.left, pid, rid, m)
-        g.remote_dma(T[kind + "p%d" % t][:, 128:192], T[sq][:, 0:64], arr, T.sem.left, pid, rid, m)
+        a, e = 128 + K * t, 128 + K * t + K
+        g.remote_dma(T[kind + "c"][:, a:e].bitcast(dt.uint8), T[cq][:, 0:64].bitcast(dt.uint8), arr, T.sem.left, pid, rid, m)
+        g.remote_dma(T[kind + "p"][:, a:e], T[sq][:, 0:64], arr, T.sem.left, pid, rid, m)
         count["left"] += 2 * len(topo.engines(core, dst))
 
     def arrival(kind, t, peer):
         n = 2 * len(topo.engines(T.cores[peer], core))
-        note("r", [], [(kind + "c%d" % t, 128, 192), (kind + "p%d" % t, 128, 192)], kind + "a%d" % t, n)
-
-    def pads(t):
-        for k in "zh":
-            quant(k + "c%d" % t, k + "p%d" % t, "zero", 0, 128)
+        a, e = 128 + K * t, 128 + K * t + K
+        note("r", [], [(kind + "c", a, e), (kind + "p", a, e)], kind + "a%d" % t, n)
 
     def as_list(row, dest, scale, base):
         op("v", lambda: V.transpose(T.ta[:, 0:256], T[row][:, 16:272]), [r(row)], [r("ta")])
@@ -162,11 +165,10 @@ def rank_program(g, core, T, topo):
         tt(T.kwf[:, 1:16:2], T.e1[:, 8:16], T.e1[:, 24:32], add, [r("e1", 8, 16), r("e1", 24, 32)], [("kwf", 8, 16)])
         ts(T[dest][:, 0:16], T.kwf[:, 0:16], scale, base, mult, add, [r("kwf")], [r(dest)])
 
-    def prekeys(first):
-        if first:
-            act(T.cm16[:, 0:256], T.cm4[:, 0:256], F.Copy, [r("cm4")], [r("cm16")], bias=2.0, scale=4.0)
-        else:
-            ts(T.cm16[:, 0:256], T.cm4[:, 0:256], 4.0, 2.0, mult, add, [r("cm4")], [r("cm16")])
+    def prekeys_own():
+        act(T.cm16[:, 0:256], T.cm4[:, 0:256], F.Copy, [r("cm4")], [r("cm16")], bias=2.0, scale=4.0)
+
+    def prekeys_next():
         tt(T.pk[:, 0:256], T.cm4[:, 0:256].indirect(T.nxo[:, 0:16]), T.cm16[:, 0:256], add, [r("cm4"), r("nxo"), r("cm16")], [r("pk")])
 
     dma("y", "du", T.ut[:], T.u[:], [], [r("ut")])
@@ -174,42 +176,47 @@ def rank_program(g, core, T, topo):
         dma("y", "dx%d" % h, T.t0[:, 512 * h:512 * h + 512], T.x[:, 512 * h:512 * h + 512], [], [r("t0", 512 * h, 512 * h + 512)])
     dma("s", "dc", T.coi[:], T.co[:], [], [r("coi")])
     dma("s", "dn", T.nxi[:], T.nx[:], [], [r("nxi")])
-    fill("ones", 0, 516, 1.0)
-    op("g", lambda: g.iota(T.mi[:, 0:64], [[1, 64]], 0, 0), [], [r("mi")])
-    op("g", lambda: g.affine_select(T.strip[:, 0:516], T.ones[:, 0:516], [[-1, 516]], AluOpType.is_equal, 0.0, 3, 4), [r("ones")], [r("strip")])
-    op("g", lambda: g.iota(T.pi[:, 0:4], [[0, 4]], 0, 1), [], [r("pi")])
-    op("g", lambda: g.iota(T.si[:, 0:4], [[16, 4]], 0, 0), [], [r("si")])
-    op("g", lambda: g.iota(T.uoi[:, 0:16], [[1, 2], [16, 8]], 0, 0), [], [r("uoi")])
-    op("g", lambda: g.iota(T.iot[:, 0:320], [[1, 320]], 0, 0, allow_small_or_imprecise_dtypes=True), [], [r("iot")])
-    ts(T.mi3[:, 0:64], T.mi[:, 0:64], 3, None, AluOpType.bitwise_and, None, [r("mi")], [r("mi3")])
-    ts(T.m4t[:, 0:64], T.mi3[:, 0:64], 4.0, None, mult, None, [r("mi3")], [r("m4t")])
-    for i in range(4):
-        fill("w%d" % i, 257, 258, 0.1875)
-        fill("fh", PL * i + C, PL * i + PL, 0.0)
-    fill("flr", 0, 256, 2.0 ** -20)
-    fill("flr", 256, 257, 0.0625)
+    fill("strip", 0, 516, 0.0)
+    whole("pif", 0, 1, [[0, 1]], 0, 1)
+    whole("iot", 0, 128, [[1, 128]])
+    whole("m4t", 0, 64, [[0, 16], [4, 4]])
+    whole("uoi", 0, 16, [[1, 2], [16, 8]])
+    whole("pi", 0, 4, [[0, 4]], 0, 1)
+    whole("si", 0, 4, [[16, 4]])
+    whole("ones", 0, 512, [[0, 512]], 1)
+    whole("iot", 128, 272, [[1, 144]], 128)
+    ts(T.strip[:, 3:515:4], T.iot[:, 0:128], T.pif[:, 0:1], None, AluOpType.is_equal, None, [r("iot", 0, 128), r("pif")], [r("strip", 3, 515)])
+    cp(T.uoo[:, 0:16], T.uoi[:, 0:16], [r("uoi")], [r("uoo")])
+    cp(T.coo[:, 0:16], T.coi[:, 0:16], [r("coi")], [r("coo")])
     for b in range(4):
         op("v", lambda: V.quantize_mx(T.eq[:, 128 * b:128 * b + 128], T.esc[:, 128 * b:128 * b + 128], T.strip[:, 3 - b:515 - b]),
            [r("strip")], [r("eq", 128 * b, 128 * b + 128), r("esc", 128 * b, 128 * b + 128)])
-    cp(T.coo[:, 0:16], T.coi[:, 0:16], [r("coi")], [r("coo")])
-    cp(T.nxo[:, 0:16], T.nxi[:, 0:16], [r("nxi")], [r("nxo")])
-    act(T.cm4[:, 0:256], T.m4t[:, 0:64].indirect(T.coo[:, 0:16]), F.Copy, [r("m4t"), r("coo")], [r("cm4")])
     ts(T.p15[:, 0:4], T.pi[:, 0:4], 15, None, AluOpType.bitwise_and, None, [r("pi")], [r("p15")])
-    cp(T.uoo[:, 0:16], T.uoi[:, 0:16], [r("uoi")], [r("uoo")])
+    act(T.cm4[:, 0:256], T.m4t[:, 0:64].indirect(T.coo[:, 0:16]), F.Copy, [r("m4t"), r("coo")], [r("cm4")])
     tt(T.kap[:, 0:4], T.p15[:, 0:4], T.si[:, 0:4], add, [r("p15"), r("si")], [r("kap")])
+    cp(T.nxo[:, 0:16], T.nxi[:, 0:16], [r("nxi")], [r("nxo")])
     quant("qu", "su", "ut", 0, 128)
-    ts(T.kv[:, 0:4], T.kap[:, 0:4], 2.0, -63.0, mult, add, [r("kap")], [r("kv")])
     cp(T.uu[:, 0:256].bitcast(dt.uint32), T.qu[:, 0:128].bitcast(dt.uint32).indirect(T.uoo[:, 0:16]), [r("qu"), r("uoo")], [r("uu")])
-    prekeys(True)
+    prekeys_own()
     act(T.us[:, 0:256], T.su[:, 0:128].indirect(T.uoo[:, 0:16]), F.Copy, [r("su"), r("uoo")], [r("us")])
     need("y", [r("t0")], [])
     dma("y", "dwc", T.wq[:, 0:512].bitcast(dt.uint8), T.wc[:, 0:2048], [], [r("wq")])
     dma("y", "dws", T.wp[:, 0:512], T.ws[:, 0:512], [], [r("wp")])
     dma("y", "dv", T.vt[:], T.v[:], [], [r("vt")])
-    for h in range(2):
-        quant("q0", "s0", "t0", 128 * h, 128, 128 * h)
-    for i in range(4):
-        cp(T["m%d" % i][:, 256:257], T.kap[:, i:i + 1], [r("kap")], [r("m%d" % i, 256, 257)])
+    quant("q0", "s0", "t0", 0, 128, 0)
+    prekeys_next()
+    ts(T.kv[:, 0:4], T.kap[:, 0:4], 2.0, -63.0, mult, add, [r("kap")], [r("kv")])
+    ts(T.nka[:, 0:1], T.kap[:, 3:4], -256.0, None, mult, None, [r("kap")], [r("nka")])
+    quant("q0", "s0", "t0", 128, 128, 128)
+    whole("ones", HOR, HOR + 1, [[0, 1]])
+    whole("lt", 64, 65, [[0, 1]], -64)
+    for b in range(4):
+        whole("fh", PL * b + C, PL * b + PL, [[0, 16]])
+        whole("zk", ZL * b, ZL * b + 1, [[0, 1]])
+    whole("zt", 256, 512, [[0, 256]])
+    for n in ("kr", "cr"):
+        whole(n, 0, 16, [[0, 16]])
+        whole(n, 272, 288, [[0, 16]])
 
     for t in range(R):
         q, s = "q%d" % t, "s%d" % t
@@ -225,138 +232,150 @@ def rank_program(g, core, T, topo):
                 bias=-1e-36, scale=-1.0)
         for a, e in ((0, 128), (128, 256)):
             tt(T.k1[:, a:e], T.sa[:, a:e], T.pk[:, a:e], add, [r("sa", a, e), r("pk", a, e)], [r("k1", a, e)])
-        for a, e in ((0, 128), (128, 256)):
             tt(T.kr[:, 16 + a:16 + e], T.k1[:, a:e], T.sb[:, a:e], mult, [r("k1", a, e), r("sb", a, e)], [r("kr", 16 + a, 16 + e)])
 
-        def half_f(b):
-            act(T.fh[:, PL * b:PL * b + C], T.pf[:, 512 * b:512 * b + C], F.Copy, [bank("pf", b)], [r("fh", PL * b, PL * b + C)], scale=0.5)
+        def plane_f(b):
+            act(T.fh[:, PL * b:PL * b + C], T.pf[:, 512 * b:512 * b + C], F.Copy, [bank("pf", b)], [r("fh", PL * b, PL * b + C)])
 
         def mask(i):
             ts(T["m%d" % i][:, 0:256], T.kr[:, 16:272], T.kv[:, i:i + 1], 2.0 ** -10, AluOpType.not_equal, amax,
                [r("kr", 16, 272), r("kv")], [r("m%d" % i, 0, 256)])
 
         def scan(i):
-            op("v", lambda: V.tensor_tensor_scan(T["w%d" % i][:, 0:257], T["m%d" % i][:, 0:257], T.flr[:, 0:257], 1.0, mult, amax),
-               [r("m%d" % i, 0, 257), r("flr", 0, 257)], [r("w%d" % i, 0, 257)])
+            if i in REV:
+                op("v", lambda: V.tensor_tensor_scan(T.ww[:, 256 * i + 255:256 * i - 1:-1], T["m%d" % i][:, 255::-1],
+                                                     T.ones[:, HOR + 255:HOR - 1:-1], 1.0, mult, add),
+                   [r("m%d" % i), r("ones", HOR, HOR + 256)], [r("ww", 256 * i, 256 * i + 256)])
+            else:
+                op("v", lambda: V.tensor_tensor_scan(T["w%d" % i][:, 0:256], T["m%d" % i][:, 0:256], T.ones[:, 0:256], 1.0, mult, mult),
+                   [r("m%d" % i), r("ones", 0, 256)], [r("w%d" % i)])
 
         def total(i):
-            if i != 2:
-                act(T.junk[:, 272 * i:272 * i + 258], T["w%d" % i][:, 0:258], F.Copy, [r("w%d" % i, 0, 258)],
-                    [r("junk", 272 * i, 272 * i + 272), r("vv", i, i + 1)], accum_out=T.vv[:, i:i + 1])
-            else:
-                op("v", lambda: V.tensor_reduce(T.vv[:, i:i + 1], T["w%d" % i][:, 0:258], AxisListType.X, add),
-                   [r("w%d" % i, 0, 258)], [r("vv", i, i + 1)])
-        half_f(0)
-        half_f(1)
+            act(T.junk[:, 256 * i:256 * i + 256], T["w%d" % i][:, 0:256], F.Copy, [r("w%d" % i)],
+                [r("junk", 256 * i, 256 * i + 256), r("ww", 256 * i, 256 * i + 1)], accum_out=T.ww[:, 256 * i:256 * i + 1])
+        plane_f(0)
+        plane_f(1)
         mask(0)
         mask(1)
         scan(0)
+        plane_f(2)
         total(0)
         mask(2)
         scan(1)
         total(1)
+        plane_f(3)
         mask(3)
         scan(2)
         scan(3)
-        total(3)
-        total(2)
-        half_f(2)
+        vv, rv = T.ww[:, 0:1024:256], [r("ww", 256 * i, 256 * i + 1) for i in range(4)]
         d = [T.si2[:, 4 * k:4 * k + 4] for k in range(5)]
         e = [r("si2", 4 * k, 4 * k + 4) for k in range(5)]
-        ts(T.f16[:, 0:4], T.vv[:, 0:4], -0.1875, None, add, None, [r("vv")], [r("f16")])
-        ts(d[0], T.vv[:, 0:4], 1024.0, None, mult, None, [r("vv")], [e[0]])
-        cp(T.fr[:, 0:64], T.iot[:, 0:320].indirect(T.f16[:, 0:4]), [r("iot"), r("f16")], [r("fr")])
-        for i in range(4):
-            act(T.jun2[:, 64 * i:64 * i + 64], T.fr[:, 0:64], F.Sign, [r("fr"), r("vv")], [r("jun2", 64 * i, 64 * i + 64), r("acc", i, i + 1)],
-                bias=T.vv[:, i:i + 1], scale=-1.0, accum_out=T.acc[:, i:i + 1])
+        cp(T.f16[:, 0:4], vv, rv, [r("f16")])
+        ts(d[0], vv, 1024.0, None, mult, None, rv, [e[0]])
+        ts(T.fr[:, 0:64], T.iot[:, 0:272].indirect(T.f16[:, 0:4]), 1.0 - 2.0 ** -10, None, mult, None, [r("iot"), r("f16")], [r("fr")])
+        for i in range(3):
+            act(T.jun2[:, 64 * i:64 * i + 64], T.fr[:, 0:64], F.Sign, [r("fr"), rv[i]], [r("jun2", 64 * i, 64 * i + 64), r("acc", i, i + 1)],
+                bias=T.ww[:, 256 * i:256 * i + 1], scale=-1.0, accum_out=T.acc[:, i:i + 1])
         for b in range(4):
-            if b == 2:
-                half_f(3)
             act(T.g1[:, 64 * b:64 * b + 64], T.fh[:, PL * b:PL * b + PL].indirect(T.f16[:, 0:4]), F.Copy,
                 [r("fh", PL * b, PL * b + PL), r("f16")], [r("g1", 64 * b, 64 * b + 64)])
 
         def mean(b):
-            tt(T.zk[:, 64 * b:64 * b + 64], T.fh[:, PL * b:PL * b + PL].indirect(T.s16[:, 0:4]), T.g1[:, 64 * b:64 * b + 64], add,
-               [r("fh", PL * b, PL * b + PL), r("s16"), r("g1", 64 * b, 64 * b + 64)], [r("zk", 64 * b, 64 * b + 64)])
+            tt(T.zk[:, ZL * b + 1:ZL * b + 65], T.fh[:, PL * b:PL * b + PL].indirect(T.s16[:, 0:4]), T.g1[:, 64 * b:64 * b + 64], add,
+               [r("fh", PL * b, PL * b + PL), r("s16"), r("g1", 64 * b, 64 * b + 64)], [r("zk", ZL * b + 1, ZL * b + 65)])
         ts(T.fi[:, 0:4], d[0], 10, None, AluOpType.arith_shift_right, None, [e[0]], [r("fi")])
         ts(d[1], d[0], 1023, None, AluOpType.bitwise_and, None, [e[0]], [e[1]])
+        ts(T.lt[:, 0:64], T.fr[:, 0:64], T.ww[:, 768:769], 2.0, AluOpType.is_lt, mult, [r("fr"), rv[3]], [r("lt", 0, 64)])
         tt(d[2], T.fi[:, 0:4], d[1], add, [r("fi"), e[1]], [e[2]])
+        op("v", lambda: V.tensor_reduce(T.acc[:, 3:4], T.lt[:, 0:65], AxisListType.X, add), [r("lt")], [r("acc", 3, 4)])
         ts(d[3], d[2], 255, None, AluOpType.bitwise_and, None, [e[2]], [e[3]])
         tt(d[4], d[3], T.fi[:, 0:4], amax, [e[3], r("fi")], [e[4]])
         ts(T.r16[:, 0:4], T.acc[:, 0:4], 0.5, 31.0, mult, add, [r("acc")], [r("r16")])
         cp(T.s16[:, 0:4], d[4], [e[4]], [r("s16")])
-        cp(T.rr[:, 0:64], T.iot[:, 0:320].indirect(T.r16[:, 0:4]), [r("iot"), r("r16")], [r("rr")])
+        cp(T.rr[:, 0:64], T.iot[:, 0:272].indirect(T.r16[:, 0:4]), [r("iot"), r("r16")], [r("rr")])
         mean(0)
         for i in range(4):
-            ts(T.om[:, 64 * i:64 * i + 64], T.rr[:, 0:64], T.kap[:, i:i + 1], None, AluOpType.not_equal, None,
-               [r("rr"), r("kap")], [r("om", 64 * i, 64 * i + 64)])
+            if i < 3:
+                ts(T.om[:, 64 * i:64 * i + 64], T.rr[:, 0:64], T.kap[:, i:i + 1], 256.0, AluOpType.not_equal, mult,
+                   [r("rr"), r("kap")], [r("om", 64 * i, 64 * i + 64)])
+            else:
+                act(T.om[:, 64 * i:64 * i + 64], T.rr[:, 0:64], F.Abs, [r("rr"), r("nka")], [r("om", 64 * i, 64 * i + 64)],
+                    bias=T.nka[:, 0:1], scale=256.0)
         mean(1)
-        op("v", lambda: V.tensor_tensor_scan(T.ow[:, 0:256], T.ones[:, 0:256], T.om[:, 0:256], 0.0, add, mult), [r("ones"), r("om")], [r("ow")])
+        op("v", lambda: V.tensor_tensor_scan(T.ow[:, 0:256], T.ones[:, 0:256], T.om[:, 0:256], 0.0, add, AluOpType.min),
+           [r("ones", 0, 256), r("om")], [r("ow")])
         mean(2)
-        ts(T.o16[:, 0:4], T.ow[:, 63:256:64], -1.0, 63.0, mult, add, [r("ow")], [r("o16")])
+        ts(T.o16[:, 0:4], T.ow[:, 63:256:64], -1.0, 64.0, mult, add, [r("ow")], [r("o16")])
         mean(3)
         for b in range(4):
-            o, i, rd, wr = T.zt[:, b:256:4], T.zk[:, 64 * b:64 * b + 64].indirect(T.o16[:, 0:4]), \
-                [r("zk", 64 * b, 64 * b + 64), r("o16")], [("zt", 64 * b, 64 * b + 64)]
+            o, i, rd, wr = T.zt[:, b:256:4], T.zk[:, ZL * b:ZL * b + 65].indirect(T.o16[:, 0:4]), \
+                [r("zk", ZL * b, ZL * b + 65), r("o16")], [("zt", 64 * b, 64 * b + 64)]
             if b < 2:
-                act(o, i, F.Copy, rd, wr)
+                act(o, i, F.Copy, rd, wr, scale=0.5)
             else:
-                cp(o, i, rd, wr)
-        if t == 0:
-            fill("zt", 256, 512, 0.0)
+                ts(o, i, 0.5, None, mult, None, rd, wr)
         quant("zq%d" % t, "zs%d" % t, "zt", 0, 128)
         send("z", t, to)
         arrival("z", t, frm)
-        for b in range(2):
-            act(T.fs[:, C * b:C * b + C], T.pf[:, 512 * b:512 * b + C], F.Copy, [bank("pf", b)], [r("fs", C * b, C * b + C)])
         if t == 0:
-            ts(T.p16[:, 0:4], T.pi[:, 0:4], 16, None, AluOpType.bitwise_and, None, [r("pi")], [r("p16")])
-            ts(T.hi[:, 0:1], T.p16[:, 0:1], 0.0625, None, mult, None, [r("p16")], [r("hi")])
-            ts(T.lo[:, 0:1], T.p16[:, 0:1], -0.0625, 1.0, mult, add, [r("p16")], [r("lo")])
-            for n in ("kr", "cr"):
-                fill(n, 0, 16, 0.0)
-                fill(n, 272, 288, 0.0)
             fill("zero", 0, 512, 0.0)
             fill("ht", 256, 512, 0.0)
-            pads(0)
+            ts(T.p16[:, 0:4], T.pi[:, 0:4], 16, None, AluOpType.bitwise_and, None, [r("pi")], [r("p16")])
+            for k in "zh":
+                quant(k + "c", k + "p", "zero", 0, 128)
+            ts(T.hi[:, 0:1], T.p16[:, 0:1], 0.0625, None, mult, None, [r("p16")], [r("hi")])
+            ts(T.lo[:, 0:1], T.p16[:, 0:1], -0.0625, 1.0, mult, add, [r("p16")], [r("lo")])
         as_list("kr", "kw", 0.5, 31.5)
         cp(T.cr[:, 16:272], T.rr[:, 0:64].indirect(T.kw[:, 0:16]), [r("rr"), r("kw")], [r("cr", 16, 272)])
-        as_list("cr", "cw", 1.0, 0.0)
-        for b in range(4):
-            mm(b, "pw", 128, "wq", "wp", 128 * b, "zc%d" % t, "zp%d" % t, 64)
-        for b in range(4):
-            act(T.ht[:, b:256:4], T.pw[:, 512 * b + 64:512 * b + 128], F.Relu, [bank("pw", b)], [("ht", 64 * b, 64 * b + 64)], scale=0.03125)
-        quant("hq%d" % t, "hs%d" % t, "ht", 0, 128)
-        send("h", t, frm)
-        arrival("h", t, to)
         if t < R - 1:
             cp(T.ri[:, 0:64], T.rr[:, 0:64], [r("rr")], [r("ri")])
             ts(T.rm[:, 0:64], T.ri[:, 0:64], 3, None, AluOpType.bitwise_and, None, [r("ri")], [r("rm")])
             ts(T.rm4[:, 0:64], T.rm[:, 0:64], 4.0, None, mult, None, [r("rm")], [r("rm4")])
-            cp(T.cm4[:, 0:256], T.rm4[:, 0:64].indirect(T.kw[:, 0:16]), [r("rm4"), r("kw")], [r("cm4")])
-            prekeys(False)
-            pads(t + 1)
+        for b in range(4):
+            mm(b, "pw", 128, "wq", "wp", 128 * b, "zc", "zp", 64 + K * t)
+        for b in range(4):
+            o, i, rd, wr = T.ht[:, b:256:4], T.pw[:, 512 * b + 64:512 * b + 128], [bank("pw", b)], [("ht", 64 * b, 64 * b + 64)]
+            if b in (1, 3):
+                ts(o, i, 0.0, 0.03125, amax, mult, rd, wr)
+            else:
+                act(o, i, F.Relu, rd, wr, scale=0.03125)
+        quant("hq%d" % t, "hs%d" % t, "ht", 0, 128)
+        send("h", t, frm)
+        arrival("h", t, to)
+        if t < R - 1:
+            act(T.cm4[:, 0:256], T.rm4[:, 0:64].indirect(T.kw[:, 0:16]), F.Copy, [r("rm4"), r("kw")], [r("cm4")])
+        as_list("cr", "cw", 1.0, 0.0)
+        if t < R - 1:
+            prekeys_own()
+            prekeys_next()
         else:
             cp(T.cf[:, 0:256], T.cr[:, 16:272], [r("cr", 16, 272)], [r("cf")])
             dma("y", "dol", T.ol[:], T.cf[0:128:16, 0:256], [r("cf")], [])
             quant("qv", "sv", "vt", 0, 128)
         new = "t%d" % (t + 1)
-        for b in (0, 2, 3, 1):
-            mm(b, "pw", 128, "eq", "esc", 128 * b, "hc%d" % t, "hp%d" % t, 64)
+        for b in range(4):
+            mm(b, "pw", 128, "eq", "esc", 128 * b, "hc", "hp", 64 + K * t)
+
+        def unpack(b):
+            o, i, rd, wr = T.dh[:, 64 * b:64 * b + 64], T.pw[:, 512 * b + 64:512 * b + 128], [bank("pw", b)], [r("dh", 64 * b, 64 * b + 64)]
+            if b == 0:
+                cp(o, i, rd, wr)
+            else:
+                act(o, i, F.Copy, rd, wr)
 
         def gather(b, h):
             o = C * (b - 2) + 128 * h
             act(T.g2[:, o:o + 128], T.dh[:, 64 * b:64 * b + 64].indirect(T.cw[:, 8 * h:8 * h + 8]), F.Copy,
                 [r("dh", 64 * b, 64 * b + 64), r("cw")], [r("g2", o, o + 128)])
-        for b in (2, 3):
-            act(T.dh[:, 64 * b:64 * b + 64], T.pw[:, 512 * b + 64:512 * b + 128], F.Copy, [bank("pw", b)], [r("dh", 64 * b, 64 * b + 64)])
-            gather(b, 0)
+        for b in range(4):
+            unpack(b)
+            if b > 1:
+                gather(b, 0)
         gather(2, 1)
         gather(3, 1)
         for b in (0, 1):
-            cp(T.dh[:, 64 * b:64 * b + 64], T.pw[:, 512 * b + 64:512 * b + 128], [bank("pw", b)], [r("dh", 64 * b, 64 * b + 64)])
-            tt(T[new][:, b:1024:4], T.dh[:, 64 * b:64 * b + 64].indirect(T.cw[:, 0:16]), T.fs[:, C * b:C * b + C], add,
-               [r("dh", 64 * b, 64 * b + 64), r("cw"), r("fs", C * b, C * b + C)], [(new, C * b, C * b + C)])
+            tt(T[new][:, b:1024:4], T.dh[:, 64 * b:64 * b + 64].indirect(T.cw[:, 0:16]), T.fh[:, PL * b:PL * b + C], add,
+               [r("dh", 64 * b, 64 * b + 64), r("cw"), r("fh", PL * b, PL * b + C)], [(new, C * b, C * b + C)])
         for h in range(2):
             for b in (2, 3):
                 o, p, w = C * (b - 2) + 128 * h, 512 * b + 128 * h, C * b + 128 * h
@@ -364,15 +383,19 @@ def rank_program(g, core, T, topo):
                    [r("g2", o, o + 128), bank("pf", b)], [(new, w, w + 128)])
             quant("q%d" % (t + 1), "s%d" % (t + 1), new, 128 * h, 128, 128 * h)
 
+    def store_scales(qu, k):
+        dma(qu, "ds%d" % k, T.osc[4 * k:4 * k + 4, 0:256], T.s3[32 * k:32 * k + 4, 0:256], [r("s3")], [])
     for h in range(2):
         dma("y", "doc%d" % h, T.oc[:, 512 * h:512 * h + 512], T.q3[:, 128 * h:128 * h + 128].bitcast(dt.uint8), [r("q3", 128 * h, 128 * h + 128)], [])
         mm(h, "pw", 128, "qv", "sv", 0, "q3", "s3", 128 * h)
     act(T.yo[:, 0:128], T.pw[:, 0:128], F.Copy, [bank("pw", 0)], [r("yo", 0, 128)])
     dma("s", "dy0", T.y[:, 0:128], T.yo[:, 0:128], [r("yo", 0, 128)], [])
     cp(T.yo[:, 128:256], T.pw[:, 512:640], [bank("pw", 1)], [r("yo", 128, 256)])
+    store_scales("y", 0)
+    store_scales("y", 1)
+    store_scales("s", 2)
     dma("s", "dy1", T.y[:, 128:256], T.yo[:, 128:256], [r("yo", 128, 256)], [])
-    for k in range(4):
-        dma("y", "ds%d" % k, T.osc[4 * k:4 * k + 4, 0:256], T.s3[32 * k:32 * k + 4, 0:256], [r("s3")], [])
+    store_scales("y", 3)
     for sname in ("cv", "cs", "ct", "cg", "left"):
         g.sync.wait_ge(T.sem[sname], count[sname])
     for sname in DMAS:

from concourse.mybir import dt, AluOpType, AxisListType, ActivationFunctionType

C, K, R = 256, 64, 3
STEP = [1, 2, 4]
PL = C + 16
ZL = K + 16
REV = (2, 3)
HOR = 256
CODES = "float8_e4m3fn_x4"

SCRATCH = {}
for _n, _w, _d in (
        ("ones", 512, "b"), ("strip", 516, "b"), ("zero", 512, "b"), ("eq", 512, "c"), ("esc", 512, "p"), ("ut", 512, "b"), ("qu", 128, "c"),
        ("su", 128, "p"), ("uu", 256, "c"), ("us", 256, "p"), ("vt", 512, "b"), ("qv", 128, "c"), ("sv", 128, "p"), ("wq", 512, "c"), ("wp", 512, "p"),
        ("nxi", 16, "i"), ("coi", 16, "i"), ("nxo", 16, "u"), ("coo", 16, "u"), ("uoi", 16, "i"), ("uoo", 16, "u"), ("iot", 272, "f"), ("pif", 1, "f"),
        ("m4t", 64, "b"), ("pi", 4, "i"), ("p15", 4, "i"), ("p16", 4, "i"), ("si", 4, "i"), ("kap", 4, "f"), ("kv", 4, "f"),
        ("lo", 1, "f"), ("hi", 1, "f"), ("nka", 1, "f"), ("fh", 4 * PL, "b"), ("sa", 256, "b"), ("sb", 256, "b"),
        ("k1", 256, "b"), ("pk", 256, "b"), ("cm4", 256, "b"), ("cm16", 256, "b"), ("kr", 288, "b"), ("cr", 288, "b"), ("ta", 256, "b"),
        ("tb", 288, "b"), ("e1", 32, "f"), ("kwf", 16, "f"), ("kw", 16, "u"), ("cw", 16, "u"), ("junk", 512, "b"), ("jun2", 256, "f"),
        ("ww", 1024, "f"), ("acc", 4, "f"), ("fr", 64, "f"), ("lt", 65, "b"), ("f16", 4, "u"), ("s16", 4, "u"), ("r16", 4, "u"), ("o16", 4, "u"),
        ("fi", 4, "i"), ("si2", 20, "i"), ("rr", 64, "b"), ("om", 256, "b"), ("ow", 256, "b"), ("g1", 256, "b"), ("zk", 4 * ZL, "b"),
        ("zt", 512, "b"), ("ht", 512, "b"), ("ri", 64, "i"), ("rm", 64, "i"), ("rm4", 64, "b"), ("dh", 256, "b"), ("g2", 512, "b"), ("cf", 256, "f"),
        ("yo", 256, "f"), ("w0", 256, "b"), ("w1", 256, "b"),
        ("zc", 128 + R * K, "c"), ("zp", 128 + R * K, "p"), ("hc", 128 + R * K, "c"), ("hp", 128 + R * K, "p")):
    SCRATCH[_n] = ("sbuf", [128, _w], {"b": "bfloat16", "c": CODES, "p": "uint8", "i": "int32", "u": "uint16", "f": "float32"}[_d])
for _n in ("pf", "pw"):
    SCRATCH[_n] = ("psum", [128, 2048], "float32")
for _i in range(4):
    SCRATCH["m%d" % _i] = ("sbuf", [128, 256], "bfloat16")
    SCRATCH["t%d" % _i] = ("sbuf", [128, 1024], "bfloat16")
    SCRATCH["q%d" % _i] = ("sbuf", [128, 256], CODES)
    SCRATCH["s%d" % _i] = ("sbuf", [128, 256], "uint8")
for _i in range(R):
    for _n in "zh":
        SCRATCH["%sq%d" % (_n, _i)] = ("sbuf", [128, 128], CODES)
        SCRATCH["%ss%d" % (_n, _i)] = ("sbuf", [128, 128], "uint8")

DMAS = ["dx0", "dx1", "du", "dv", "dwc", "dws", "dn", "dc", "dol", "dy0", "dy1", "doc0", "doc1", "ds0", "ds1", "ds2", "ds3"]
SEMAPHORES = ["cv", "cs", "ct", "cg", "left"] + ["za%d" % i for i in range(R)] + ["ha%d" % i for i in range(R)] + DMAS


def rank_program(g, core, T, topo):
    rank = T.rank_of(core)
    if rank is None:
        return
    add, mult, amax = AluOpType.add, AluOpType.mult, AluOpType.max
    F = ActivationFunctionType
    eng = {"v": g.vector, "s": g.scalar, "t": g.tensor, "g": g, "y": g.sync}
    count = {"cv": 0, "cs": 0, "ct": 0, "cg": 0, "left": 0}
    known = {q: {} for q in eng}
    wrote, read = {}, {}

    def over(book, reg):
        return [e for e in book.get(reg[0], []) if e[0] < reg[2] and reg[1] < e[1]]

    def need(q, reads, writes):
        want = {}
        for reg in reads:
            for e in over(wrote, reg):
                want[e[3]] = max(want.get(e[3], 0), e[4])
            if reg[0] in ("pf", "pw"):
                for e in over(read, reg):
                    if e[2] != q:
                        want[e[3]] = max(want.get(e[3], 0), e[4])
        for reg in writes:
            for e in over(wrote, reg):
                want[e[3]] = max(want.get(e[3], 0), e[4])
            for e in over(read, reg):
                if e[2] != q:
                    want[e[3]] = max(want.get(e[3], 0), e[4])
        for s in sorted(want):
            if known[q].get(s, 0) < want[s]:
                eng[q].wait_ge(T.sem[s], want[s])
                known[q][s] = want[s]

    def note(q, reads, writes, s, n):
        for reg in writes:
            for book in (wrote, read):
                book[reg[0]] = [e for e in book.get(reg[0], []) if not (reg[1] <= e[0] and e[1] <= reg[2])]
            wrote[reg[0]].append((reg[1], reg[2], q, s, n))
        for reg in reads:
            book = [e for e in read.get(reg[0], []) if not (e[2] == q and reg[1] <= e[0] and e[1] <= reg[2])]
            book.append((reg[1], reg[2], q, s, n))
            read[reg[0]] = book

    def op(q, call, reads, writes):
        need(q, reads, writes)
        s = "c" + q
        count[s] += 1
        call().then_inc(T.sem[s], 1)
        note(q, reads, writes, s, count[s])

    def dma(q, s, out, in_, reads, writes):
        need(q, reads, writes)
        eng[q].dma_start(out, in_).then_inc(T.sem[s], 16)
        note(q, reads, writes, s, 16)

    V, S, PE = g.vector, g.scalar, g.tensor

    def r(name, a=0, b=None):
        return (name, a, T[name].shape[1] if b is None else b)

    def quant(qb, sb_, tile, a, n, c0=0):
        if tile == "t0":
            src = [(tile, 4 * c0, 4 * (c0 + n))]
        elif tile in ("t1", "t2", "t3"):
            src = [(tile, C * b + c0, C * b + c0 + n) for b in range(4)]
        else:
            src = [r(tile)]
        op("v", lambda: V.quantize_mx(T[qb][:, a:a + n], T[sb_][:, a:a + n], T[tile][:, 4 * c0:4 * (c0 + n)]),
           src, [r(qb, a, a + n), r(sb_, a, a + n)])

    def fill(name, a, b, val):
        op("v", lambda: V.memset(T[name][:, a:b], val), [], [r(name, a, b)])

    def whole(name, a, b, pattern, base=0, per=0):
        op("g", lambda: g.iota(T[name][:, a:b], pattern, base, per, allow_small_or_imprecise_dtypes=True), [], [r(name, a, b)])

    def ts(out, in0, s1, s2, op0, op1, reads, writes):
        if s2 is None:
            op("v", lambda: V.tensor_scalar(out, in0, s1, None, op0), reads, writes)
        else:
            op("v", lambda: V.tensor_scalar(out, in0, s1, s2, op0, op1), reads, writes)

    def tt(out, a, b, o, reads, writes):
        op("v", lambda: V.tensor_tensor(out, a, b, o), reads, writes)

    def cp(out, a, reads, writes):
        op("v", lambda: V.tensor_copy(out, a), reads, writes)

    def act(out, a, f, reads, writes, **kw):
        op("s", lambda: S.activation(out, a, f, **kw), reads, writes)

    def mm(bank, buf, n, lq, ls, la, rq, rs, ra):
        op("t", lambda: PE.matmul_mx(T[buf][:, 512 * bank:512 * bank + n], T[lq][:, la:la + 128], T[ls][:, la:la + 128],
                                     T[rq][:, ra:ra + n], T[rs][:, ra:ra + n], True, True),
           [r(lq, la, la + 128), r(ls, la, la + 128), r(rq, ra, ra + n), r(rs, ra, ra + n)], [(buf, 512 * bank, 512 * bank + 512)])

    def bank(buf, b):
        return (buf, 512 * b, 512 * b + 512)

    def send(kind, t, peer):
        cq, sq = kind + "q%d" % t, kind + "s%d" % t
        need("g", [r(cq, 0, 64), r(sq, 0, 64)], [])
        dst = T.cores[peer]
        rid, pid, _se = topo.addr(dst)
        m, arr = topo.mask(core, dst), T.sem[kind + "a%d" % t]
        a, e = 128 + K * t, 128 + K * t + K
        g.remote_dma(T[kind + "c"][:, a:e].bitcast(dt.uint8), T[cq][:, 0:64].bitcast(dt.uint8), arr, T.sem.left, pid, rid, m)
        g.remote_dma(T[kind + "p"][:, a:e], T[sq][:, 0:64], arr, T.sem.left, pid, rid, m)
        count["left"] += 2 * len(topo.engines(core, dst))

    def arrival(kind, t, peer):
        n = 2 * len(topo.engines(T.cores[peer], core))
        a, e = 128 + K * t, 128 + K * t + K
        note("r", [], [(kind + "c", a, e), (kind + "p", a, e)], kind + "a%d" % t, n)

    def as_list(row, dest, scale, base):
        op("v", lambda: V.transpose(T.ta[:, 0:256], T[row][:, 16:272]), [r(row)], [r("ta")])
        op("v", lambda: V.transpose(T.tb[:, 0:288], T[row][:, 0:288]), [r(row)], [r("tb")])
        for k, (src, a, m) in enumerate((("ta", 0, "lo"), ("ta", 16, "hi"), ("tb", 16, "hi"), ("tb", 32, "lo"))):
            end = 288 if a == 32 else 256
            ts(T.e1[:, 8 * k:8 * k + 8], T[src][:, a:end:32], T[m][:, 0:1], None, mult, None, [r(src), r(m)], [r("e1", 8 * k, 8 * k + 8)])
        tt(T.kwf[:, 0:16:2], T.e1[:, 0:8], T.e1[:, 16:24], add, [r("e1", 0, 8), r("e1", 16, 24)], [("kwf", 0, 8)])
        tt(T.kwf[:, 1:16:2], T.e1[:, 8:16], T.e1[:, 24:32], add, [r("e1", 8, 16), r("e1", 24, 32)], [("kwf", 8, 16)])
        ts(T[dest][:, 0:16], T.kwf[:, 0:16], scale, base, mult, add, [r("kwf")], [r(dest)])

    def prekeys_own():
        act(T.cm16[:, 0:256], T.cm4[:, 0:256], F.Copy, [r("cm4")], [r("cm16")], bias=2.0, scale=4.0)

    def prekeys_next():
        tt(T.pk[:, 0:256], T.cm4[:, 0:256].indirect(T.nxo[:, 0:16]), T.cm16[:, 0:256], add, [r("cm4"), r("nxo"), r("cm16")], [r("pk")])

    dma("y", "du", T.ut[:], T.u[:], [], [r("ut")])
    for h in range(2):
        dma("y", "dx%d" % h, T.t0[:, 512 * h:512 * h + 512], T.x[:, 512 * h:512 * h + 512], [], [r("t0", 512 * h, 512 * h + 512)])
    dma("s", "dc", T.coi[:], T.co[:], [], [r("coi")])
    dma("s", "dn", T.nxi[:], T.nx[:], [], [r("nxi")])
    fill("strip", 0, 516, 0.0)
    whole("pif", 0, 1, [[0, 1]], 0, 1)
    whole("iot", 0, 128, [[1, 128]])
    whole("m4t", 0, 64, [[0, 16], [4, 4]])
    whole("uoi", 0, 16, [[1, 2], [16, 8]])
    whole("pi", 0, 4, [[0, 4]], 0, 1)
    whole("si", 0, 4, [[16, 4]])
    whole("ones", 0, 512, [[0, 512]], 1)
    whole("iot", 128, 272, [[1, 144]], 128)
    ts(T.strip[:, 3:515:4], T.iot[:, 0:128], T.pif[:, 0:1], None, AluOpType.is_equal, None, [r("iot", 0, 128), r("pif")], [r("strip", 3, 515)])
    cp(T.uoo[:, 0:16], T.uoi[:, 0:16], [r("uoi")], [r("uoo")])
    cp(T.coo[:, 0:16], T.coi[:, 0:16], [r("coi")], [r("coo")])
    for b in range(4):
        op("v", lambda: V.quantize_mx(T.eq[:, 128 * b:128 * b + 128], T.esc[:, 128 * b:128 * b + 128], T.strip[:, 3 - b:515 - b]),
           [r("strip")], [r("eq", 128 * b, 128 * b + 128), r("esc", 128 * b, 128 * b + 128)])
    ts(T.p15[:, 0:4], T.pi[:, 0:4], 15, None, AluOpType.bitwise_and, None, [r("pi")], [r("p15")])
    act(T.cm4[:, 0:256], T.m4t[:, 0:64].indirect(T.coo[:, 0:16]), F.Copy, [r("m4t"), r("coo")], [r("cm4")])
    tt(T.kap[:, 0:4], T.p15[:, 0:4], T.si[:, 0:4], add, [r("p15"), r("si")], [r("kap")])
    cp(T.nxo[:, 0:16], T.nxi[:, 0:16], [r("nxi")], [r("nxo")])
    quant("qu", "su", "ut", 0, 128)
    cp(T.uu[:, 0:256].bitcast(dt.uint32), T.qu[:, 0:128].bitcast(dt.uint32).indirect(T.uoo[:, 0:16]), [r("qu"), r("uoo")], [r("uu")])
    prekeys_own()
    act(T.us[:, 0:256], T.su[:, 0:128].indirect(T.uoo[:, 0:16]), F.Copy, [r("su"), r("uoo")], [r("us")])
    need("y", [r("t0")], [])
    dma("y", "dwc", T.wq[:, 0:512].bitcast(dt.uint8), T.wc[:, 0:2048], [], [r("wq")])
    dma("y", "dws", T.wp[:, 0:512], T.ws[:, 0:512], [], [r("wp")])
    dma("y", "dv", T.vt[:], T.v[:], [], [r("vt")])
    quant("q0", "s0", "t0", 0, 128, 0)
    prekeys_next()
    ts(T.kv[:, 0:4], T.kap[:, 0:4], 2.0, -63.0, mult, add, [r("kap")], [r("kv")])
    ts(T.nka[:, 0:1], T.kap[:, 3:4], -256.0, None, mult, None, [r("kap")], [r("nka")])
    quant("q0", "s0", "t0", 128, 128, 128)
    whole("ones", HOR, HOR + 1, [[0, 1]])
    whole("lt", 64, 65, [[0, 1]], -64)
    for b in range(4):
        whole("fh", PL * b + C, PL * b + PL, [[0, 16]])
        whole("zk", ZL * b, ZL * b + 1, [[0, 1]])
    whole("zt", 256, 512, [[0, 256]])
    for n in ("kr", "cr"):
        whole(n, 0, 16, [[0, 16]])
        whole(n, 272, 288, [[0, 16]])

    for t in range(R):
        q, s = "q%d" % t, "s%d" % t
        to, frm = (rank + STEP[t]) % len(T.cores), (rank - STEP[t]) % len(T.cores)
        for h in range(2):
            for k in range(2):
                mm(2 * h + k, "pw", 128, "uu", "us", 128 * k, q, s, 128 * h)
        for b in range(4):
            mm(b, "pf", 256, "eq", "esc", 128 * b, q, s, 0)
        for h, k in ((0, 0), (0, 1), (1, 0), (1, 1)):
            n, a, e = ("sa", "sb")[k], 128 * h, 128 * h + 128
            act(T[n][:, a:e], T.pw[:, 1024 * h + 512 * k:1024 * h + 512 * k + 128], F.Sign, [bank("pw", 2 * h + k)], [r(n, a, e)],
                bias=-1e-36, scale=-1.0)
        for a, e in ((0, 128), (128, 256)):
            tt(T.k1[:, a:e], T.sa[:, a:e], T.pk[:, a:e], add, [r("sa", a, e), r("pk", a, e)], [r("k1", a, e)])
            tt(T.kr[:, 16 + a:16 + e], T.k1[:, a:e], T.sb[:, a:e], mult, [r("k1", a, e), r("sb", a, e)], [r("kr", 16 + a, 16 + e)])

        def plane_f(b):
            act(T.fh[:, PL * b:PL * b + C], T.pf[:, 512 * b:512 * b + C], F.Copy, [bank("pf", b)], [r("fh", PL * b, PL * b + C)])

        def mask(i):
            ts(T["m%d" % i][:, 0:256], T.kr[:, 16:272], T.kv[:, i:i + 1], 2.0 ** -10, AluOpType.not_equal, amax,
               [r("kr", 16, 272), r("kv")], [r("m%d" % i, 0, 256)])

        def scan(i):
            if i in REV:
                op("v", lambda: V.tensor_tensor_scan(T.ww[:, 256 * i + 255:256 * i - 1:-1], T["m%d" % i][:, 255::-1],
                                                     T.ones[:, HOR + 255:HOR - 1:-1], 1.0, mult, add),
                   [r("m%d" % i), r("ones", HOR, HOR + 256)], [r("ww", 256 * i, 256 * i + 256)])
            else:
                op("v", lambda: V.tensor_tensor_scan(T["w%d" % i][:, 0:256], T["m%d" % i][:, 0:256], T.ones[:, 0:256], 1.0, mult, mult),
                   [r("m%d" % i), r("ones", 0, 256)], [r("w%d" % i)])

        def total(i):
            act(T.junk[:, 256 * i:256 * i + 256], T["w%d" % i][:, 0:256], F.Copy, [r("w%d" % i)],
                [r("junk", 256 * i, 256 * i + 256), r("ww", 256 * i, 256 * i + 1)], accum_out=T.ww[:, 256 * i:256 * i + 1])
        plane_f(0)
        plane_f(1)
        mask(0)
        mask(1)
        scan(0)
        plane_f(2)
        total(0)
        mask(2)
        scan(1)
        total(1)
        plane_f(3)
        mask(3)
        scan(2)
        scan(3)
        vv, rv = T.ww[:, 0:1024:256], [r("ww", 256 * i, 256 * i + 1) for i in range(4)]
        d = [T.si2[:, 4 * k:4 * k + 4] for k in range(5)]
        e = [r("si2", 4 * k, 4 * k + 4) for k in range(5)]
        cp(T.f16[:, 0:4], vv, rv, [r("f16")])
        ts(d[0], vv, 1024.0, None, mult, None, rv, [e[0]])
        ts(T.fr[:, 0:64], T.iot[:, 0:272].indirect(T.f16[:, 0:4]), 1.0 - 2.0 ** -10, None, mult, None, [r("iot"), r("f16")], [r("fr")])
        for i in range(3):
            act(T.jun2[:, 64 * i:64 * i + 64], T.fr[:, 0:64], F.Sign, [r("fr"), rv[i]], [r("jun2", 64 * i, 64 * i + 64), r("acc", i, i + 1)],
                bias=T.ww[:, 256 * i:256 * i + 1], scale=-1.0, accum_out=T.acc[:, i:i + 1])
        for b in range(4):
            act(T.g1[:, 64 * b:64 * b + 64], T.fh[:, PL * b:PL * b + PL].indirect(T.f16[:, 0:4]), F.Copy,
                [r("fh", PL * b, PL * b + PL), r("f16")], [r("g1", 64 * b, 64 * b + 64)])

        def mean(b):
            tt(T.zk[:, ZL * b + 1:ZL * b + 65], T.fh[:, PL * b:PL * b + PL].indirect(T.s16[:, 0:4]), T.g1[:, 64 * b:64 * b + 64], add,
               [r("fh", PL * b, PL * b + PL), r("s16"), r("g1", 64 * b, 64 * b + 64)], [r("zk", ZL * b + 1, ZL * b + 65)])
        ts(T.fi[:, 0:4], d[0], 10, None, AluOpType.arith_shift_right, None, [e[0]], [r("fi")])
        ts(d[1], d[0], 1023, None, AluOpType.bitwise_and, None, [e[0]], [e[1]])
        ts(T.lt[:, 0:64], T.fr[:, 0:64], T.ww[:, 768:769], 2.0, AluOpType.is_lt, mult, [r("fr"), rv[3]], [r("lt", 0, 64)])
        tt(d[2], T.fi[:, 0:4], d[1], add, [r("fi"), e[1]], [e[2]])
        op("v", lambda: V.tensor_reduce(T.acc[:, 3:4], T.lt[:, 0:65], AxisListType.X, add), [r("lt")], [r("acc", 3, 4)])
        ts(d[3], d[2], 255, None, AluOpType.bitwise_and, None, [e[2]], [e[3]])
        tt(d[4], d[3], T.fi[:, 0:4], amax, [e[3], r("fi")], [e[4]])
        ts(T.r16[:, 0:4], T.acc[:, 0:4], 0.5, 31.0, mult, add, [r("acc")], [r("r16")])
        cp(T.s16[:, 0:4], d[4], [e[4]], [r("s16")])
        cp(T.rr[:, 0:64], T.iot[:, 0:272].indirect(T.r16[:, 0:4]), [r("iot"), r("r16")], [r("rr")])
        mean(0)
        for i in range(4):
            if i < 3:
                ts(T.om[:, 64 * i:64 * i + 64], T.rr[:, 0:64], T.kap[:, i:i + 1], 256.0, AluOpType.not_equal, mult,
                   [r("rr"), r("kap")], [r("om", 64 * i, 64 * i + 64)])
            else:
                act(T.om[:, 64 * i:64 * i + 64], T.rr[:, 0:64], F.Abs, [r("rr"), r("nka")], [r("om", 64 * i, 64 * i + 64)],
                    bias=T.nka[:, 0:1], scale=256.0)
        mean(1)
        op("v", lambda: V.tensor_tensor_scan(T.ow[:, 0:256], T.ones[:, 0:256], T.om[:, 0:256], 0.0, add, AluOpType.min),
           [r("ones", 0, 256), r("om")], [r("ow")])
        mean(2)
        ts(T.o16[:, 0:4], T.ow[:, 63:256:64], -1.0, 64.0, mult, add, [r("ow")], [r("o16")])
        mean(3)
        for b in range(4):
            o, i, rd, wr = T.zt[:, b:256:4], T.zk[:, ZL * b:ZL * b + 65].indirect(T.o16[:, 0:4]), \
                [r("zk", ZL * b, ZL * b + 65), r("o16")], [("zt", 64 * b, 64 * b + 64)]
            if b < 2:
                act(o, i, F.Copy, rd, wr, scale=0.5)
            else:
                ts(o, i, 0.5, None, mult, None, rd, wr)
        quant("zq%d" % t, "zs%d" % t, "zt", 0, 128)
        send("z", t, to)
        arrival("z", t, frm)
        if t == 0:
            fill("zero", 0, 512, 0.0)
            fill("ht", 256, 512, 0.0)
            ts(T.p16[:, 0:4], T.pi[:, 0:4], 16, None, AluOpType.bitwise_and, None, [r("pi")], [r("p16")])
            for k in "zh":
                quant(k + "c", k + "p", "zero", 0, 128)
            ts(T.hi[:, 0:1], T.p16[:, 0:1], 0.0625, None, mult, None, [r("p16")], [r("hi")])
            ts(T.lo[:, 0:1], T.p16[:, 0:1], -0.0625, 1.0, mult, add, [r("p16")], [r("lo")])
        as_list("kr", "kw", 0.5, 31.5)
        cp(T.cr[:, 16:272], T.rr[:, 0:64].indirect(T.kw[:, 0:16]), [r("rr"), r("kw")], [r("cr", 16, 272)])
        if t < R - 1:
            cp(T.ri[:, 0:64], T.rr[:, 0:64], [r("rr")], [r("ri")])
            ts(T.rm[:, 0:64], T.ri[:, 0:64], 3, None, AluOpType.bitwise_and, None, [r("ri")], [r("rm")])
            ts(T.rm4[:, 0:64], T.rm[:, 0:64], 4.0, None, mult, None, [r("rm")], [r("rm4")])
        for b in range(4):
            mm(b, "pw", 128, "wq", "wp", 128 * b, "zc", "zp", 64 + K * t)
        for b in range(4):
            o, i, rd, wr = T.ht[:, b:256:4], T.pw[:, 512 * b + 64:512 * b + 128], [bank("pw", b)], [("ht", 64 * b, 64 * b + 64)]
            if b in (1, 3):
                ts(o, i, 0.0, 0.03125, amax, mult, rd, wr)
            else:
                act(o, i, F.Relu, rd, wr, scale=0.03125)
        quant("hq%d" % t, "hs%d" % t, "ht", 0, 128)
        send("h", t, frm)
        arrival("h", t, to)
        if t < R - 1:
            act(T.cm4[:, 0:256], T.rm4[:, 0:64].indirect(T.kw[:, 0:16]), F.Copy, [r("rm4"), r("kw")], [r("cm4")])
        as_list("cr", "cw", 1.0, 0.0)
        if t < R - 1:
            prekeys_own()
            prekeys_next()
        else:
            cp(T.cf[:, 0:256], T.cr[:, 16:272], [r("cr", 16, 272)], [r("cf")])
            dma("y", "dol", T.ol[:], T.cf[0:128:16, 0:256], [r("cf")], [])
            quant("qv", "sv", "vt", 0, 128)
        new = "t%d" % (t + 1)
        for b in range(4):
            mm(b, "pw", 128, "eq", "esc", 128 * b, "hc", "hp", 64 + K * t)

        def unpack(b):
            o, i, rd, wr = T.dh[:, 64 * b:64 * b + 64], T.pw[:, 512 * b + 64:512 * b + 128], [bank("pw", b)], [r("dh", 64 * b, 64 * b + 64)]
            if b == 0:
                cp(o, i, rd, wr)
            else:
                act(o, i, F.Copy, rd, wr)

        def gather(b, h):
            o = C * (b - 2) + 128 * h
            act(T.g2[:, o:o + 128], T.dh[:, 64 * b:64 * b + 64].indirect(T.cw[:, 8 * h:8 * h + 8]), F.Copy,
                [r("dh", 64 * b, 64 * b + 64), r("cw")], [r("g2", o, o + 128)])
        for b in range(4):
            unpack(b)
            if b > 1:
                gather(b, 0)
        gather(2, 1)
        gather(3, 1)
        for b in (0, 1):
            tt(T[new][:, b:1024:4], T.dh[:, 64 * b:64 * b + 64].indirect(T.cw[:, 0:16]), T.fh[:, PL * b:PL * b + C], add,
               [r("dh", 64 * b, 64 * b + 64), r("cw"), r("fh", PL * b, PL * b + C)], [(new, C * b, C * b + C)])
        for h in range(2):
            for b in (2, 3):
                o, p, w = C * (b - 2) + 128 * h, 512 * b + 128 * h, C * b + 128 * h
                tt(T[new][:, 512 * h + b:512 * h + 512:4], T.g2[:, o:o + 128], T.pf[:, p:p + 128], add,
                   [r("g2", o, o + 128), bank("pf", b)], [(new, w, w + 128)])
            quant("q%d" % (t + 1), "s%d" % (t + 1), new, 128 * h, 128, 128 * h)

    def store_scales(qu, k):
        dma(qu, "ds%d" % k, T.osc[4 * k:4 * k + 4, 0:256], T.s3[32 * k:32 * k + 4, 0:256], [r("s3")], [])
    for h in range(2):
        dma("y", "doc%d" % h, T.oc[:, 512 * h:512 * h + 512], T.q3[:, 128 * h:128 * h + 128].bitcast(dt.uint8), [r("q3", 128 * h, 128 * h + 128)], [])
        mm(h, "pw", 128, "qv", "sv", 0, "q3", "s3", 128 * h)
    act(T.yo[:, 0:128], T.pw[:, 0:128], F.Copy, [bank("pw", 0)], [r("yo", 0, 128)])
    dma("s", "dy0", T.y[:, 0:128], T.yo[:, 0:128], [r("yo", 0, 128)], [])
    cp(T.yo[:, 128:256], T.pw[:, 512:640], [bank("pw", 1)], [r("yo", 128, 256)])
    store_scales("y", 0)
    store_scales("y", 1)
    store_scales("s", 2)
    dma("s", "dy1", T.y[:, 128:256], T.yo[:, 128:256], [r("yo", 128, 256)], [])
    store_scales("y", 3)
    for sname in ("cv", "cs", "ct", "cg", "left"):
        g.sync.wait_ge(T.sem[sname], count[sname])
    for sname in DMAS:
        if known["y"].get(sname, 0) < 16:
            g.sync.wait_ge(T.sem[sname], 16)
